import numpy as np
import ml_dtypes


def mxq(x, axis, fmt="e4m3"):
    dtype, down = {"e4m3": (ml_dtypes.float8_e4m3fn, 7), "e5m2": (ml_dtypes.float8_e5m2, 14)}[fmt]
    v = np.moveaxis(np.asarray(x, np.float32).astype(ml_dtypes.bfloat16).astype(np.float64), axis, -1)
    blocks = v.reshape(v.shape[:-1] + (-1, 32))
    amax = np.abs(blocks).max(-1, keepdims=True)
    byte = np.maximum(np.where(amax > 0, np.frexp(amax)[1] - 1 + 127, 0) - down, 1)
    scale = np.exp2(byte - 127.0)
    codes = (blocks / scale).astype(np.float32).astype(dtype).astype(np.float64)
    return np.moveaxis((codes * scale).reshape(v.shape), -1, axis)


WIDE = False


def mx_kscale(k):
    if not WIDE:
        return np.ones(k)
    levels = np.array([10, -10, 5, -5, 0])
    if k % 512:
        return np.exp2(np.random.permutation(np.resize(levels, k // 32))).repeat(32)
    a = np.empty((k // 512, 16))
    for p in range(k // 512):
        a[p, :8] = np.random.permutation(np.resize(levels, 8))
        for g in range(8):
            far = levels[np.abs(levels - a[p, g]) >= 10]
            a[p, g + 8] = far[np.random.randint(len(far))]
    return np.exp2(a.ravel()).repeat(32)


BF16 = ml_dtypes.bfloat16


def bf(x):
    return np.asarray(x, np.float32).astype(BF16)


def f64(x):
    return np.asarray(x).astype(np.float64)

def planes(Y):
    n, m = Y.shape
    b = f64(bf(Y)).reshape(n // 32, 32, m)
    amax = np.abs(b).max(1)
    byte = np.clip(np.where(amax > 0, np.frexp(amax)[1] - 1 + 127 - 7, 1), 1, 254)
    codes = (b * np.exp2(127.0 - byte)[:, None, :]).reshape(n, m).astype(np.float32).astype(ml_dtypes.float8_e4m3fn).view(np.uint8)
    words = codes.reshape(n // 512, 128, 4, m).transpose(0, 1, 3, 2)
    return np.ascontiguousarray(words), np.ascontiguousarray(byte.astype(np.uint8).reshape(n // 512, 16, m))


K, M, N, D = 2, 512, 1024, 1024


def root_curvature(u):
    p = 1.0 / (1.0 + np.exp(-u))
    return np.sqrt(p * (1.0 - p))


def setup_inputs():
    s = mx_kscale(N)
    t = mx_kscale(K * M).reshape(K, M)
    x = np.random.standard_normal((K, N, D)) * (12.0 / np.sqrt(K * N))
    u = np.random.standard_normal((K, N)) * 2.0
    sk = np.random.standard_normal((K, M, N)) / np.sqrt(M)
    a = 1.0 + 0.3 * np.random.standard_normal((K, M))
    b = 1.0 + 0.3 * np.random.standard_normal((K, M))
    return {"x": bf(x / s[None, :, None]), "u": bf(u), "sk": bf(sk * s[None, None, :]), "a": bf(a * t), "b": bf(b / t)}


def core(x, u, sk, a, b):
    c = root_curvature(f64(u))
    q = c[:, :, None] * f64(x)
    y = mxq(f64(sk), 2, "e4m3") @ mxq(q, 1, "e4m3")
    left = (f64(a)[:, :, None] * y).reshape(K * M, D)
    right = (f64(b)[:, :, None] * y).reshape(K * M, D)
    return mxq(left, 0, "e4m3").T @ mxq(right, 0, "e4m3")


def reference(x, u, sk, a, b):
    R_out = core(x, u, sk, a, b)
    words, scales = planes(R_out.T)
    return R_out, words, scales

@@ -1,0 +1,442 @@
+from contextlib import ExitStack
+
+import concourse.mybir as mybir
+from concourse.masks import make_identity
+
+K, M, N, D = 2, 512, 1024, 1024
+FLOPS = 2 * K * M * N * D + 2 * K * M * D * D
+
+F32 = mybir.dt.float32
+BF16 = mybir.dt.bfloat16
+U32 = mybir.dt.uint32
+I32 = mybir.dt.int32
+U8 = mybir.dt.uint8
+FP8X4 = mybir.dt.float8_e4m3fn_x4
+ACT = mybir.ActivationFunctionType
+ALU = mybir.AluOpType
+
+P = 128
+PACK = 4
+G = N // (P * PACK)
+HALF = 512
+NH = D // HALF
+SUB = 128
+NS = HALF // SUB
+
+MULT_ON_GPSIMD = ((1, 1, 0), (0, 0, 1), (0, 1, 1), (1, 0, 1), (1, 1, 1))
+
+
+def tile_federatednewtonsketchlogistichessian_x1_kernel(tc, x, u, sk, a, b, out, words, scales):
+    nc = tc.nc
+    with ExitStack() as ctx:
+        keep = ctx.enter_context(tc.tile_pool(name="keep", bufs=1))
+        mul_pool = ctx.enter_context(tc.tile_pool(name="mul", bufs=4))
+        grp_pool = ctx.enter_context(tc.tile_pool(name="grp", bufs=4))
+        lr_pool = ctx.enter_context(tc.tile_pool(name="lr", bufs=2))
+        out_pool = ctx.enter_context(tc.tile_pool(name="outp", bufs=6))
+        psum = ctx.enter_context(tc.psum_pool(name="psum", bufs=2))
+        ctx.enter_context(tc.manual_schedule())
+
+        u_sb = keep.tile([P, K * G, PACK], BF16, name="u_sb")
+        a_sb = keep.tile([P, K, PACK], BF16, name="a_sb")
+        b_sb = keep.tile([P, K, PACK], BF16, name="b_sb")
+        nc.sync.dma_start(out=u_sb[:], in_=u.rearrange("k (g p j) -> p (k g) j", g=G, j=PACK))
+        x_raw = {}
+        sk_raw = {}
+
+        def load_x(k, g, h):
+            t = keep.tile([P, PACK, HALF], BF16, name=f"x_{k}{g}{h}", align_bytes=64)
+            nc.sync.dma_start(
+                out=t[:],
+                in_=x[k, 512 * g : 512 * g + 512, HALF * h : HALF * h + HALF].rearrange("(p j) d -> p j d", j=PACK),
+            )
+            x_raw[k, g, h] = t
+
+        def load_sk(k, half):
+            t = keep.tile([P, 2, N], BF16, name=f"sk_{k}{half}", align_bytes=64)
+            nc.sync.dma_start(
+                out=t[:], in_=sk[k].rearrange("(m t) n -> m t n", t=PACK)[:, 2 * half : 2 * half + 2, :]
+            )
+            sk_raw[k, half] = t
+
+        load_x(0, 0, 0)
+        load_sk(0, 0)
+        load_sk(0, 1)
+        load_x(0, 1, 0)
+        nc.sync.dma_start(out=a_sb[:], in_=a.rearrange("k (p t) -> p k t", t=PACK))
+        nc.sync.dma_start(out=b_sb[:], in_=b.rearrange("k (p t) -> p k t", t=PACK))
+        load_x(1, 0, 0)
+        load_x(1, 1, 0)
+        load_sk(1, 0)
+        load_sk(1, 1)
+        load_x(0, 0, 1)
+        load_x(0, 1, 1)
+        load_x(1, 0, 1)
+        load_x(1, 1, 1)
+
+        ident = keep.tile([P, P], F32, name="ident")
+        make_identity(nc, ident[:])
+
+        warm = keep.tile([P, 1], F32, name="warm")
+        nc.vector.memset(warm[:], 0.0)
+        warm2 = keep.tile([P, 1], F32, name="warm2")
+        nc.scalar.activation(out=warm2[:], in_=warm[:], func=ACT.Exp)
+        na = keep.tile([P, K * G, PACK], F32, name="na")
+        e1 = keep.tile([P, K * G, PACK], F32, name="e1")
+        e2 = keep.tile([P, K * G, PACK], F32, name="e2")
+        rec = keep.tile([P, K * G, PACK], F32, name="rec")
+        c_sb = keep.tile([P, K * G, PACK], F32, name="c_sb")
+        nc.vector.scalar_tensor_tensor(out=na[:], in0=u_sb[:], scalar=-1.0, in1=u_sb[:], op0=ALU.mult, op1=ALU.min)
+        nc.scalar.activation(out=e2[:], in_=na[:], func=ACT.Exp)
+        nc.scalar.activation(out=e1[:], in_=na[:], func=ACT.Exp, scale=0.5)
+        nc.vector.tensor_scalar_add(out=e2[:], in0=e2[:], scalar1=1.0)
+        nc.vector.reciprocal(out=rec[:], in_=e2[:])
+        nc.vector.tensor_tensor(out=c_sb[:], in0=rec[:], in1=e1[:], op=ALU.mult)
+
+        q_mul = {}
+        q_codes = {}
+        q_scales = {}
+        s_codes = {}
+        s_scales = {}
+        s_grp = {}
+
+        def mult(k, g, h):
+            t = mul_pool.tile([P, PACK, HALF], BF16, name="qm", align_bytes=64)
+            q_mul[k, g, h] = t
+            for j in range(PACK):
+                cj = c_sb[:, k * G + g, j : j + 1]
+                if (k, g, h) in MULT_ON_GPSIMD:
+                    nc.gpsimd.tensor_scalar(
+                        out=t[:, j, :], in0=x_raw[k, g, h][:, j, :], scalar1=cj, scalar2=0.0, op0=ALU.mult, op1=ALU.add
+                    )
+                else:
+                    nc.vector.tensor_scalar_mul(out=t[:, j, :], in0=x_raw[k, g, h][:, j, :], scalar1=cj)
+
+        q_grp = {}
+
+        def inter(k, g, h, d0=0, d1=HALF, on_vector=False):
+            if d0 == 0:
+                q_grp[k, g, h] = grp_pool.tile([P, HALF, PACK], BF16, name="qg", align_bytes=64)
+            dst = q_grp[k, g, h][:, d0:d1, :].rearrange("p (c i) t -> p c t i", i=4)
+            src = q_mul[k, g, h][:, :, d0:d1].rearrange("p t (c i) -> p c t i", i=4)
+            if on_vector:
+                nc.vector.tensor_copy(out=dst, in_=src)
+            else:
+                nc.scalar.copy(out=dst, in_=src)
+
+        def quant_q(k, g, h, d0=0, d1=HALF):
+            if d0 == 0:
+                q_codes[k, g, h] = keep.tile([P, HALF], U32, name=f"qc_{k}{g}{h}", align_bytes=64)
+                q_scales[k, g, h] = keep.tile([P, HALF], U8, name=f"qs_{k}{g}{h}", align_bytes=64)
+            nc.vector.quantize_mx(
+                out=q_codes[k, g, h][:, d0:d1].bitcast(FP8X4),
+                scales=q_scales[k, g, h][:, d0:d1],
+                in_=q_grp[k, g, h][:, d0:d1, :].rearrange("p d t -> p (d t)"),
+            )
+
+        def sk_turn(k, half, g, tag, on_vector):
+            if half == 0:
+                s_grp[k, g] = grp_pool.tile([P, M, PACK], BF16, name=f"sg{g}", bufs=2, align_bytes=64)
+            xt = psum.tile([P, 2, 2, P], F32, name="xt", tag=tag, bufs=6 if tag == "b" else 2)
+            for tt in range(2):
+                w = sk_raw[k, half][:, tt, :].bitcast(F32)
+                for e in range(2):
+                    nc.tensor.transpose(xt[:, tt, e, :], w[:, 256 * g + e : 256 * (g + 1) : 2], ident[:])
+            dst = s_grp[k, g][:, 256 * half : 256 * half + 256, :].rearrange("p m t -> p (m t)").bitcast(F32)
+            dst = dst.rearrange("p (t m e) -> p t m e", t=2, e=2)
+            src = xt[:].rearrange("p t e m -> p t m e")
+            if on_vector:
+                nc.vector.tensor_copy(out=dst, in_=src)
+            else:
+                nc.scalar.copy(out=dst, in_=src)
+
+        def quant_s(k, g):
+            codes = keep.tile([P, M], U32, name=f"sc_{k}{g}", align_bytes=64)
+            sc = keep.tile([P, M], U8, name=f"ss_{k}{g}", align_bytes=64)
+            nc.vector.quantize_mx(
+                out=codes[:].bitcast(FP8X4), scales=sc[:], in_=s_grp[k, g][:].rearrange("p m t -> p (m t)")
+            )
+            s_codes[k, g] = codes
+            s_scales[k, g] = sc
+
+        y_bank = {}
+
+        def stage1(k, h, s):
+            bank = psum.tile([P, PACK, SUB], F32, name="yb", tag="b", bufs=6)
+            y_bank[k, h, s] = bank
+            cols = slice(SUB * s, SUB * s + SUB)
+            for t in range(PACK):
+                mc = slice(P * t, P * t + P)
+                for g in range(G):
+                    nc.tensor.matmul_mx(
+                        out=bank[:, t, :],
+                        lhsT=s_codes[k, g][:, mc].bitcast(FP8X4),
+                        lhsT_scale=s_scales[k, g][:, mc],
+                        rhs=q_codes[k, g, h][:, cols].bitcast(FP8X4),
+                        rhs_scale=q_scales[k, g, h][:, cols],
+                        start=(g == 0),
+                        stop=(g == G - 1),
+                    )
+
+        lr = {}
+        lr_codes = {}
+        lr_scales = {}
+        for side in range(2):
+            for k in range(K):
+                lr_codes[side, k] = keep.tile([P, D], U32, name=f"lrc_{side}{k}", align_bytes=64)
+                lr_scales[side, k] = keep.tile([P, D], U8, name=f"lrs_{side}{k}", align_bytes=64)
+
+        def weigh(k, h, s):
+            for side in range(2):
+                if s == 0:
+                    lr[side, k, h] = lr_pool.tile([P, HALF, PACK], BF16, name=f"lr{side}", align_bytes=64)
+                wt = (a_sb, b_sb)[side]
+                nc.vector.tensor_tensor(
+                    out=lr[side, k, h][:, SUB * s : SUB * s + SUB, :],
+                    in0=y_bank[k, h, s][:].rearrange("p t d -> p d t"),
+                    in1=wt[:, k : k + 1, :].to_broadcast([P, SUB, PACK]),
+                    op=ALU.mult,
+                )
+
+        def quant_lr(side, k, h, s0, s1):
+            cols = slice(HALF * h + SUB * s0, HALF * h + SUB * s1)
+            nc.vector.quantize_mx(
+                out=lr_codes[side, k][:, cols].bitcast(FP8X4),
+                scales=lr_scales[side, k][:, cols],
+                in_=lr[side, k, h][:, SUB * s0 : SUB * s1, :].rearrange("p d t -> p (d t)"),
+            )
+
+        o_bank = {}
+        o_f32 = {}
+        o_bf = {}
+
+        def stage2(i, c0, c1):
+            width = c1 - c0
+            banks = []
+            for ii in range(2):
+                if ii == 0 or width == HALF:
+                    bank = psum.tile([P, HALF], F32, name="ob", tag="b", bufs=6)
+                    banks.append(bank)
+                rows = slice(P * (i + ii), P * (i + ii) + P)
+                lo = 0 if width == HALF else width * ii
+                for k in range(K):
+                    nc.tensor.matmul_mx(
+                        out=bank[:, lo : lo + width],
+                        lhsT=lr_codes[0, k][:, rows].bitcast(FP8X4),
+                        lhsT_scale=lr_scales[0, k][:, rows],
+                        rhs=lr_codes[1, k][:, c0:c1].bitcast(FP8X4),
+                        rhs_scale=lr_scales[1, k][:, c0:c1],
+                        start=(k == 0),
+                        stop=(k == K - 1),
+                    )
+            o_bank[i, c0] = banks
+
+        def emit_out(i, c0, c1, engines="ss", store=True):
+            f = c0 // HALF
+            if (i, f) not in o_f32:
+                o_f32[i, f] = out_pool.tile([P, 2, HALF], F32, name="o32", bufs=8, align_bytes=64)
+                o_bf[i, f] = out_pool.tile([P, 2, 2, P, 2], BF16, name="o16", bufs=8, align_bytes=64)
+            lo, hi = c0 - HALF * f, c1 - HALF * f
+            banks = o_bank[i, c0]
+            for n, bank in enumerate(banks):
+                if len(banks) == 2:
+                    dst, src = o_f32[i, f][:, n, lo:hi], bank[:]
+                else:
+                    dst, src = o_f32[i, f][:, :, lo:hi], bank[:].rearrange("p (i c) -> p i c", i=2)
+                if engines[n] == "v":
+                    nc.vector.tensor_copy(out=dst, in_=src)
+                else:
+                    nc.scalar.copy(out=dst, in_=src)
+            if store:
+                store_out(i, c0, c1)
+
+        def store_out(i, c0, c1):
+            f = c0 // HALF
+            lo, hi = c0 - HALF * f, c1 - HALF * f
+            nc.sync.dma_start(
+                out=out[P * i : P * i + 2 * P, c0:c1].rearrange("(i p) c -> p i c", i=2), in_=o_f32[i, f][:, :, lo:hi]
+            )
+
+        def round_out(i, c0, c1, eng):
+            f = c0 // HALF
+            lo, hi = c0 - HALF * f, c1 - HALF * f
+            for ii in range(2):
+                dst = o_bf[i, f][:, ii, :, lo // 4 : hi // 4, :]
+                src = o_f32[i, f][:, ii, lo:hi].rearrange("p (m u e) -> p u m e", u=2, e=2)
+                if eng == "g":
+                    nc.gpsimd.tensor_scalar(out=dst, in0=src, scalar1=1.0, scalar2=0.0, op0=ALU.mult, op1=ALU.add)
+                else:
+                    nc.vector.tensor_copy(out=dst, in_=src)
+
+        pl_codes = {}
+        pl_scales = {}
+        for f in range(NH):
+            pl_codes[f] = keep.tile([P, D], U32, name=f"plc_{f}", align_bytes=64)
+            pl_scales[f] = keep.tile([P, D], U8, name=f"pls_{f}", align_bytes=64)
+
+        pl_grp = {}
+
+        def plane_turn(i, f, on_vector):
+            xt = psum.tile([P, 2, 2, P], F32, name="pt", tag="tr")
+            for ii in range(2):
+                for e in range(2):
+                    w = o_bf[i, f][:, ii, e, :, :].rearrange("p m e -> p (m e)").bitcast(F32)
+                    nc.tensor.transpose(xt[:, ii, e, :], w, ident[:])
+            grp = out_pool.tile([P, 2 * P, PACK], BF16, name="pg", bufs=4, align_bytes=64)
+            pl_grp[i, f] = grp
+            dst = grp[:].rearrange("p d t -> p (d t)").bitcast(F32).rearrange("p (i d e) -> p i d e", i=2, e=2)
+            src = xt[:].rearrange("p i e d -> p i d e")
+            if on_vector:
+                nc.vector.tensor_copy(out=dst, in_=src)
+            else:
+                nc.scalar.copy(out=dst, in_=src)
+
+        def plane_quant(i, f):
+            cols = slice(P * i, P * i + 2 * P)
+            nc.vector.quantize_mx(
+                out=pl_codes[f][:, cols].bitcast(FP8X4),
+                scales=pl_scales[f][:, cols],
+                in_=pl_grp[i, f][:].rearrange("p d t -> p (d t)"),
+            )
+
+        def plane_store_words(f, i0, i1):
+            nc.sync.dma_start(
+                out=words[f, :, P * i0 : P * i1, :].rearrange("p d t -> p (d t)").bitcast(I32),
+                in_=pl_codes[f][:, P * i0 : P * i1].bitcast(I32),
+            )
+
+        def plane_store_scales(f):
+            for q in range(4):
+                nc.sync.dma_start(
+                    out=scales[f, 4 * q : 4 * q + 4, :].bitcast(I32),
+                    in_=pl_scales[f][32 * q : 32 * q + 4, :].bitcast(I32),
+                )
+
+        mult(0, 0, 0)
+        sk_turn(0, 0, 0, "b", False)
+        sk_turn(0, 0, 1, "b", False)
+        inter(0, 0, 0, 0, 512, True)
+        sk_turn(0, 1, 0, "b", False)
+        sk_turn(0, 1, 1, "b", False)
+        quant_q(0, 0, 0)
+        mult(0, 1, 0)
+        quant_s(0, 0)
+        inter(0, 1, 0, 0, 256, True)
+        inter(0, 1, 0, 256, 512)
+        quant_s(0, 1)
+        quant_q(0, 1, 0, 0, 256)
+        quant_q(0, 1, 0, 256, 512)
+        mult(1, 0, 0)
+        mult(1, 1, 0)
+        inter(1, 0, 0)
+        for s in range(NS):
+            stage1(0, 0, s)
+        sk_turn(1, 0, 0, "tr", False)
+        sk_turn(1, 0, 1, "tr", False)
+        for s in range(NS):
+            weigh(0, 0, s)
+        sk_turn(1, 1, 0, "b", False)
+        sk_turn(1, 1, 1, "b", False)
+        inter(1, 1, 0)
+        quant_lr(0, 0, 0, 0, 4)
+        quant_lr(1, 0, 0, 0, 4)
+        quant_q(1, 0, 0)
+        quant_s(1, 0)
+        quant_s(1, 1)
+        quant_q(1, 1, 0)
+        mult(0, 0, 1)
+        mult(0, 1, 1)
+        for s in range(NS):
+            stage1(1, 0, s)
+        inter(0, 0, 1)
+        inter(0, 1, 1)
+        mult(1, 0, 1)
+        mult(1, 1, 1)
+        for s in range(NS):
+            weigh(1, 0, s)
+        quant_lr(0, 1, 0, 0, 4)
+        quant_lr(1, 1, 0, 0, 4)
+        quant_q(0, 0, 1)
+        quant_q(0, 1, 1)
+        inter(1, 0, 1)
+        for s in range(2):
+            stage1(0, 1, s)
+        inter(1, 1, 1)
+        stage2(0, 0, 512)
+        emit_out(0, 0, 512)
+        round_out(0, 0, 512, "g")
+        stage2(2, 0, 512)
+        emit_out(2, 0, 512)
+        round_out(2, 0, 512, "g")
+        quant_q(1, 0, 1)
+        weigh(0, 1, 0)
+        weigh(0, 1, 1)
+        quant_q(1, 1, 1)
+        quant_lr(0, 0, 1, 0, 2)
+        quant_lr(1, 0, 1, 0, 2)
+        stage1(1, 1, 0)
+        stage1(1, 1, 1)
+        plane_turn(0, 0, False)
+        stage1(0, 1, 2)
+        stage1(0, 1, 3)
+        plane_turn(2, 0, False)
+        weigh(1, 1, 0)
+        weigh(1, 1, 1)
+        weigh(0, 1, 2)
+        quant_lr(0, 1, 1, 0, 2)
+        quant_lr(1, 1, 1, 0, 2)
+        stage1(1, 1, 2)
+        stage1(1, 1, 3)
+        weigh(0, 1, 3)
+        plane_quant(0, 0)
+        plane_quant(2, 0)
+        plane_store_words(0, 0, 4)
+        stage2(4, 0, 512)
+        emit_out(4, 0, 512)
+        round_out(4, 0, 512, "g")
+        quant_lr(0, 0, 1, 2, 4)
+        quant_lr(1, 0, 1, 2, 4)
+        weigh(1, 1, 2)
+        for i in (0, 2, 4):
+            stage2(i, 512, 768)
+            emit_out(i, 512, 768)
+            round_out(i, 512, 768, "g")
+        plane_turn(4, 0, False)
+        weigh(1, 1, 3)
+        quant_lr(0, 1, 1, 2, 4)
+        quant_lr(1, 1, 1, 2, 4)
+        stage2(6, 0, 512)
+        stage2(0, 768, 1024)
+        stage2(2, 768, 1024)
+        emit_out(6, 0, 512, "sv")
+        emit_out(0, 768, 1024)
+        plane_quant(4, 0)
+        round_out(6, 0, 512, "v")
+        emit_out(2, 768, 1024)
+        round_out(0, 768, 1024, "v")
+        plane_turn(6, 0, True)
+        stage2(4, 768, 1024)
+        emit_out(4, 768, 1024)
+        round_out(2, 768, 1024, "v")
+        plane_turn(0, 1, False)
+        plane_quant(6, 0)
+        plane_store_words(0, 4, 8)
+        plane_store_scales(0)
+        stage2(6, 512, 768)
+        stage2(6, 768, 1024)
+        round_out(4, 768, 1024, "v")
+        emit_out(6, 512, 768, store=False)
+        emit_out(6, 768, 1024, store=False)
+        store_out(6, 512, 1024)
+        plane_turn(2, 1, True)
+        plane_quant(0, 1)
+        round_out(6, 512, 768, "v")
+        plane_quant(2, 1)
+        plane_store_words(1, 0, 4)
+        round_out(6, 768, 1024, "v")
+        plane_turn(4, 1, False)
+        plane_turn(6, 1, True)
+        plane_quant(4, 1)
+        plane_quant(6, 1)
+        plane_store_words(1, 4, 8)
+        plane_store_scales(1)

@@ -23,7 +23,7 @@ NH = D // HALF
 SUB = 128
 NS = HALF // SUB
 
-MULT_ON_GPSIMD = ((1, 1, 0), (0, 0, 1), (0, 1, 1), (1, 0, 1), (1, 1, 1))
+MULT_ON_GPSIMD = ()
 
 
 def tile_federatednewtonsketchlogistichessian_x1_kernel(tc, x, u, sk, a, b, out, words, scales):
@@ -327,33 +327,37 @@ def tile_federatednewtonsketchlogistichessian_x1_kernel(tc, x, u, sk, a, b, out,
         quant_q(0, 1, 0, 0, 256)
         quant_q(0, 1, 0, 256, 512)
         mult(1, 0, 0)
-        mult(1, 1, 0)
         inter(1, 0, 0)
         for s in range(NS):
             stage1(0, 0, s)
         sk_turn(1, 0, 0, "tr", False)
         sk_turn(1, 0, 1, "tr", False)
-        for s in range(NS):
-            weigh(0, 0, s)
+        weigh(0, 0, 0)
+        weigh(0, 0, 1)
+        mult(1, 1, 0)
+        weigh(0, 0, 2)
+        weigh(0, 0, 3)
         sk_turn(1, 1, 0, "b", False)
         sk_turn(1, 1, 1, "b", False)
         inter(1, 1, 0)
         quant_lr(0, 0, 0, 0, 4)
         quant_lr(1, 0, 0, 0, 4)
         quant_q(1, 0, 0)
+        mult(0, 0, 1)
         quant_s(1, 0)
         quant_s(1, 1)
         quant_q(1, 1, 0)
-        mult(0, 0, 1)
         mult(0, 1, 1)
         for s in range(NS):
             stage1(1, 0, s)
         inter(0, 0, 1)
         inter(0, 1, 1)
+        weigh(1, 0, 0)
+        weigh(1, 0, 1)
         mult(1, 0, 1)
+        weigh(1, 0, 2)
+        weigh(1, 0, 3)
         mult(1, 1, 1)
-        for s in range(NS):
-            weigh(1, 0, s)
         quant_lr(0, 1, 0, 0, 4)
         quant_lr(1, 1, 0, 0, 4)
         quant_q(0, 0, 1)
@@ -364,10 +368,8 @@ def tile_federatednewtonsketchlogistichessian_x1_kernel(tc, x, u, sk, a, b, out,
         inter(1, 1, 1)
         stage2(0, 0, 512)
         emit_out(0, 0, 512)
-        round_out(0, 0, 512, "g")
         stage2(2, 0, 512)
         emit_out(2, 0, 512)
-        round_out(2, 0, 512, "g")
         quant_q(1, 0, 1)
         weigh(0, 1, 0)
         weigh(0, 1, 1)
@@ -376,11 +378,13 @@ def tile_federatednewtonsketchlogistichessian_x1_kernel(tc, x, u, sk, a, b, out,
         quant_lr(1, 0, 1, 0, 2)
         stage1(1, 1, 0)
         stage1(1, 1, 1)
-        plane_turn(0, 0, False)
+        round_out(0, 0, 512, "v")
         stage1(0, 1, 2)
+        plane_turn(0, 0, False)
         stage1(0, 1, 3)
-        plane_turn(2, 0, False)
         weigh(1, 1, 0)
+        round_out(2, 0, 512, "v")
+        plane_turn(2, 0, False)
         weigh(1, 1, 1)
         weigh(0, 1, 2)
         quant_lr(0, 1, 1, 0, 2)
@@ -393,14 +397,13 @@ def tile_federatednewtonsketchlogistichessian_x1_kernel(tc, x, u, sk, a, b, out,
         plane_store_words(0, 0, 4)
         stage2(4, 0, 512)
         emit_out(4, 0, 512)
-        round_out(4, 0, 512, "g")
         quant_lr(0, 0, 1, 2, 4)
         quant_lr(1, 0, 1, 2, 4)
         weigh(1, 1, 2)
         for i in (0, 2, 4):
             stage2(i, 512, 768)
             emit_out(i, 512, 768)
-            round_out(i, 512, 768, "g")
+        round_out(4, 0, 512, "v")
         plane_turn(4, 0, False)
         weigh(1, 1, 3)
         quant_lr(0, 1, 1, 2, 4)
@@ -413,27 +416,26 @@ def tile_federatednewtonsketchlogistichessian_x1_kernel(tc, x, u, sk, a, b, out,
         plane_quant(4, 0)
         round_out(6, 0, 512, "v")
         emit_out(2, 768, 1024)
-        round_out(0, 768, 1024, "v")
+        round_out(0, 512, 1024, "v")
         plane_turn(6, 0, True)
         stage2(4, 768, 1024)
         emit_out(4, 768, 1024)
-        round_out(2, 768, 1024, "v")
+        round_out(2, 512, 1024, "v")
         plane_turn(0, 1, False)
         plane_quant(6, 0)
         plane_store_words(0, 4, 8)
         plane_store_scales(0)
         stage2(6, 512, 768)
         stage2(6, 768, 1024)
-        round_out(4, 768, 1024, "v")
+        round_out(4, 512, 1024, "v")
         emit_out(6, 512, 768, store=False)
         emit_out(6, 768, 1024, store=False)
         store_out(6, 512, 1024)
         plane_turn(2, 1, True)
         plane_quant(0, 1)
-        round_out(6, 512, 768, "v")
         plane_quant(2, 1)
         plane_store_words(1, 0, 4)
-        round_out(6, 768, 1024, "v")
+        round_out(6, 512, 1024, "v")
         plane_turn(4, 1, False)
         plane_turn(6, 1, True)
         plane_quant(4, 1)

@@ -37,10 +37,9 @@ def tile_federatednewtonsketchlogistichessian_x1_kernel(tc, x, u, sk, a, b, out,
         psum = ctx.enter_context(tc.psum_pool(name="psum", bufs=2))
         ctx.enter_context(tc.manual_schedule())
 
-        u_sb = keep.tile([P, K * G, PACK], BF16, name="u_sb")
-        a_sb = keep.tile([P, K, PACK], BF16, name="a_sb")
-        b_sb = keep.tile([P, K, PACK], BF16, name="b_sb")
-        nc.sync.dma_start(out=u_sb[:], in_=u.rearrange("k (g p j) -> p (k g) j", g=G, j=PACK))
+        rows = keep.tile([P, M], BF16, name="rows", align_bytes=64)
+        nc.vector.memset(rows[:], 0.0)
+        nc.sync.dma_start(out=rows[0 : K * G, :], in_=u.rearrange("k (g n) -> (k g) n", g=G))
         x_raw = {}
         sk_raw = {}
 
@@ -59,12 +58,12 @@ def tile_federatednewtonsketchlogistichessian_x1_kernel(tc, x, u, sk, a, b, out,
             )
             sk_raw[k, half] = t
 
+        nc.sync.dma_start(out=rows[4:6, :], in_=a)
+        nc.sync.dma_start(out=rows[6:8, :], in_=b)
         load_x(0, 0, 0)
         load_sk(0, 0)
         load_sk(0, 1)
         load_x(0, 1, 0)
-        nc.sync.dma_start(out=a_sb[:], in_=a.rearrange("k (p t) -> p k t", t=PACK))
-        nc.sync.dma_start(out=b_sb[:], in_=b.rearrange("k (p t) -> p k t", t=PACK))
         load_x(1, 0, 0)
         load_x(1, 1, 0)
         load_sk(1, 0)
@@ -81,17 +80,29 @@ def tile_federatednewtonsketchlogistichessian_x1_kernel(tc, x, u, sk, a, b, out,
         nc.vector.memset(warm[:], 0.0)
         warm2 = keep.tile([P, 1], F32, name="warm2")
         nc.scalar.activation(out=warm2[:], in_=warm[:], func=ACT.Exp)
-        na = keep.tile([P, K * G, PACK], F32, name="na")
+        au = keep.tile([P, K * G, PACK], F32, name="au")
+        ab_sb = keep.tile([P, 2 * K, PACK], F32, name="ab_sb")
         e1 = keep.tile([P, K * G, PACK], F32, name="e1")
         e2 = keep.tile([P, K * G, PACK], F32, name="e2")
         rec = keep.tile([P, K * G, PACK], F32, name="rec")
         c_sb = keep.tile([P, K * G, PACK], F32, name="c_sb")
-        nc.vector.scalar_tensor_tensor(out=na[:], in0=u_sb[:], scalar=-1.0, in1=u_sb[:], op0=ALU.mult, op1=ALU.min)
-        nc.scalar.activation(out=e2[:], in_=na[:], func=ACT.Exp)
-        nc.scalar.activation(out=e1[:], in_=na[:], func=ACT.Exp, scale=0.5)
+        rw = rows[:].bitcast(F32)
+
+        row_bank = psum.tile([P, 2, P], F32, name="ut", tag="tr", bufs=2)
+        for e in range(2):
+            nc.tensor.transpose(row_bank[:, e, :], rw[:, e : M // 2 : 2], ident[:])
+        u_t = row_bank[:].bitcast(BF16).rearrange("p e (r f) -> p r e f", f=2)
+        nc.scalar.activation(
+            out=au[:].rearrange("p r (e f) -> p r e f", f=2), in_=u_t[:, 0:4, :, :], func=ACT.Abs
+        )
+        nc.scalar.activation(out=e2[:], in_=au[:], func=ACT.Exp, scale=-1.0)
+        nc.scalar.activation(out=e1[:], in_=au[:], func=ACT.Exp, scale=-0.5)
         nc.vector.tensor_scalar_add(out=e2[:], in0=e2[:], scalar1=1.0)
         nc.vector.reciprocal(out=rec[:], in_=e2[:])
         nc.vector.tensor_tensor(out=c_sb[:], in0=rec[:], in1=e1[:], op=ALU.mult)
+
+        def make_ab():
+            nc.vector.tensor_copy(out=ab_sb[:].rearrange("p r (e f) -> p r e f", f=2), in_=u_t[:, 4:8, :, :])
 
         q_mul = {}
         q_codes = {}
@@ -186,17 +197,26 @@ def tile_federatednewtonsketchlogistichessian_x1_kernel(tc, x, u, sk, a, b, out,
                 lr_codes[side, k] = keep.tile([P, D], U32, name=f"lrc_{side}{k}", align_bytes=64)
                 lr_scales[side, k] = keep.tile([P, D], U8, name=f"lrs_{side}{k}", align_bytes=64)
 
-        def weigh(k, h, s):
-            for side in range(2):
-                if s == 0:
+        def weigh(k, h, s, sides=(0, 1), on_scalar=False):
+            for side in sides:
+                if s == 0 and (side, k, h) not in lr:
                     lr[side, k, h] = lr_pool.tile([P, HALF, PACK], BF16, name=f"lr{side}", align_bytes=64)
-                wt = (a_sb, b_sb)[side]
-                nc.vector.tensor_tensor(
-                    out=lr[side, k, h][:, SUB * s : SUB * s + SUB, :],
-                    in0=y_bank[k, h, s][:].rearrange("p t d -> p d t"),
-                    in1=wt[:, k : k + 1, :].to_broadcast([P, SUB, PACK]),
-                    op=ALU.mult,
-                )
+                dst = lr[side, k, h][:, SUB * s : SUB * s + SUB, :]
+                row = K * side + k
+                if on_scalar:
+                    tmp = lr_pool.tile([P, PACK, SUB], BF16, name="wt", align_bytes=64)
+                    for t in range(PACK):
+                        nc.scalar.activation(
+                            out=tmp[:, t, :], in_=y_bank[k, h, s][:, t, :], func=ACT.Copy, scale=ab_sb[:, row, t : t + 1]
+                        )
+                    nc.scalar.copy(out=dst, in_=tmp[:].rearrange("p t d -> p d t"))
+                else:
+                    nc.vector.tensor_tensor(
+                        out=dst,
+                        in0=y_bank[k, h, s][:].rearrange("p t d -> p d t"),
+                        in1=ab_sb[:, row : row + 1, :].to_broadcast([P, SUB, PACK]),
+                        op=ALU.mult,
+                    )
 
         def quant_lr(side, k, h, s0, s1):
             cols = slice(HALF * h + SUB * s0, HALF * h + SUB * s1)
@@ -262,17 +282,21 @@ def tile_federatednewtonsketchlogistichessian_x1_kernel(tc, x, u, sk, a, b, out,
             lo, hi = c0 - HALF * f, c1 - HALF * f
             for ii in range(2):
                 dst = o_bf[i, f][:, ii, :, lo // 4 : hi // 4, :]
-                src = o_f32[i, f][:, ii, lo:hi].rearrange("p (m u e) -> p u m e", u=2, e=2)
-                if eng == "g":
-                    nc.gpsimd.tensor_scalar(out=dst, in0=src, scalar1=1.0, scalar2=0.0, op0=ALU.mult, op1=ALU.add)
+                if eng == "s":
+                    banks = o_bank[i, c0]
+                    src = banks[ii][:] if len(banks) == 2 else banks[0][:, (hi - lo) * ii : (hi - lo) * (ii + 1)]
+                    nc.scalar.copy(out=dst, in_=src.rearrange("p (m u e) -> p u m e", u=2, e=2))
                 else:
+                    src = o_f32[i, f][:, ii, lo:hi].rearrange("p (m u e) -> p u m e", u=2, e=2)
                     nc.vector.tensor_copy(out=dst, in_=src)
 
         pl_codes = {}
         pl_scales = {}
         for f in range(NH):
             pl_codes[f] = keep.tile([P, D], U32, name=f"plc_{f}", align_bytes=64)
-            pl_scales[f] = keep.tile([P, D], U8, name=f"pls_{f}", align_bytes=64)
+        pl_scale_tile = keep.tile([P, NH, D], U8, name="pls", align_bytes=64)
+        for f in range(NH):
+            pl_scales[f] = pl_scale_tile[:, f, :]
 
         pl_grp = {}
 
@@ -305,14 +329,15 @@ def tile_federatednewtonsketchlogistichessian_x1_kernel(tc, x, u, sk, a, b, out,
                 in_=pl_codes[f][:, P * i0 : P * i1].bitcast(I32),
             )
 
-        def plane_store_scales(f):
+        def plane_store_scales():
             for q in range(4):
                 nc.sync.dma_start(
-                    out=scales[f, 4 * q : 4 * q + 4, :].bitcast(I32),
-                    in_=pl_scales[f][32 * q : 32 * q + 4, :].bitcast(I32),
+                    out=scales[:, 4 * q : 4 * q + 4, :].bitcast(I32).rearrange("f r m -> r f m"),
+                    in_=pl_scale_tile[32 * q : 32 * q + 4, :, :].bitcast(I32),
                 )
 
         mult(0, 0, 0)
+        make_ab()
         sk_turn(0, 0, 0, "b", False)
         sk_turn(0, 0, 1, "b", False)
         inter(0, 0, 0, 0, 512, True)
@@ -325,8 +350,8 @@ def tile_federatednewtonsketchlogistichessian_x1_kernel(tc, x, u, sk, a, b, out,
         inter(0, 1, 0, 256, 512)
         quant_s(0, 1)
         quant_q(0, 1, 0, 0, 256)
-        quant_q(0, 1, 0, 256, 512)
         mult(1, 0, 0)
+        quant_q(0, 1, 0, 256, 512)
         inter(1, 0, 0)
         for s in range(NS):
             stage1(0, 0, s)
@@ -343,8 +368,8 @@ def tile_federatednewtonsketchlogistichessian_x1_kernel(tc, x, u, sk, a, b, out,
         quant_lr(0, 0, 0, 0, 4)
         quant_lr(1, 0, 0, 0, 4)
         quant_q(1, 0, 0)
-        mult(0, 0, 1)
         quant_s(1, 0)
+        mult(0, 0, 1)
         quant_s(1, 1)
         quant_q(1, 1, 0)
         mult(0, 1, 1)
@@ -355,90 +380,91 @@ def tile_federatednewtonsketchlogistichessian_x1_kernel(tc, x, u, sk, a, b, out,
         weigh(1, 0, 0)
         weigh(1, 0, 1)
         mult(1, 0, 1)
+        quant_q(0, 0, 1)
         weigh(1, 0, 2)
-        weigh(1, 0, 3)
         mult(1, 1, 1)
+        quant_q(0, 1, 1)
+        stage1(0, 1, 0)
+        stage1(0, 1, 1)
+        weigh(1, 0, 3)
+        inter(1, 0, 1)
+        inter(1, 1, 1)
         quant_lr(0, 1, 0, 0, 4)
         quant_lr(1, 1, 0, 0, 4)
-        quant_q(0, 0, 1)
-        quant_q(0, 1, 1)
-        inter(1, 0, 1)
-        for s in range(2):
-            stage1(0, 1, s)
-        inter(1, 1, 1)
-        stage2(0, 0, 512)
-        emit_out(0, 0, 512)
-        stage2(2, 0, 512)
-        emit_out(2, 0, 512)
-        quant_q(1, 0, 1)
         weigh(0, 1, 0)
         weigh(0, 1, 1)
-        quant_q(1, 1, 1)
+        quant_q(1, 0, 1)
+        for i in (0, 2):
+            stage2(i, 0, 512)
+            emit_out(i, 0, 512)
+            round_out(i, 0, 512, "s")
         quant_lr(0, 0, 1, 0, 2)
         quant_lr(1, 0, 1, 0, 2)
+        quant_q(1, 1, 1)
+        stage1(0, 1, 2)
+        stage1(0, 1, 3)
+        weigh(0, 1, 2)
         stage1(1, 1, 0)
         stage1(1, 1, 1)
-        round_out(0, 0, 512, "v")
-        stage1(0, 1, 2)
-        plane_turn(0, 0, False)
-        stage1(0, 1, 3)
         weigh(1, 1, 0)
-        round_out(2, 0, 512, "v")
-        plane_turn(2, 0, False)
         weigh(1, 1, 1)
-        weigh(0, 1, 2)
+        plane_turn(0, 0, False)
+        plane_turn(2, 0, False)
         quant_lr(0, 1, 1, 0, 2)
         quant_lr(1, 1, 1, 0, 2)
         stage1(1, 1, 2)
-        stage1(1, 1, 3)
         weigh(0, 1, 3)
-        plane_quant(0, 0)
-        plane_quant(2, 0)
-        plane_store_words(0, 0, 4)
         stage2(4, 0, 512)
         emit_out(4, 0, 512)
+        stage2(0, 512, 768)
+        emit_out(0, 512, 768)
+        stage1(1, 1, 3)
         quant_lr(0, 0, 1, 2, 4)
         quant_lr(1, 0, 1, 2, 4)
-        weigh(1, 1, 2)
-        for i in (0, 2, 4):
+        weigh(1, 1, 2, (0,))
+        weigh(1, 1, 3, (0,))
+        for i in (2, 4):
             stage2(i, 512, 768)
             emit_out(i, 512, 768)
-        round_out(4, 0, 512, "v")
-        plane_turn(4, 0, False)
-        weigh(1, 1, 3)
+        plane_quant(0, 0)
         quant_lr(0, 1, 1, 2, 4)
-        quant_lr(1, 1, 1, 2, 4)
+        weigh(1, 1, 2, (1,))
+        weigh(1, 1, 3, (1,))
+        plane_quant(2, 0)
+        plane_store_words(0, 0, 4)
         stage2(6, 0, 512)
+        emit_out(6, 0, 512)
+        stage2(6, 512, 768)
+        emit_out(6, 512, 768, store=False)
+        quant_lr(1, 1, 1, 2, 4)
+        round_out(4, 0, 512, "v")
         stage2(0, 768, 1024)
         stage2(2, 768, 1024)
-        emit_out(6, 0, 512, "sv")
         emit_out(0, 768, 1024)
-        plane_quant(4, 0)
         round_out(6, 0, 512, "v")
+        plane_turn(4, 0, True)
         emit_out(2, 768, 1024)
-        round_out(0, 512, 1024, "v")
-        plane_turn(6, 0, True)
         stage2(4, 768, 1024)
+        round_out(0, 512, 1024, "v")
         emit_out(4, 768, 1024)
-        round_out(2, 512, 1024, "v")
-        plane_turn(0, 1, False)
-        plane_quant(6, 0)
-        plane_store_words(0, 4, 8)
-        plane_store_scales(0)
-        stage2(6, 512, 768)
+        plane_turn(6, 0, True)
         stage2(6, 768, 1024)
-        round_out(4, 512, 1024, "v")
-        emit_out(6, 512, 768, store=False)
+        round_out(2, 512, 1024, "v")
+        plane_quant(4, 0)
+        plane_turn(0, 1, False)
         emit_out(6, 768, 1024, store=False)
         store_out(6, 512, 1024)
-        plane_turn(2, 1, True)
+        plane_quant(6, 0)
+        plane_store_words(0, 4, 8)
+        round_out(4, 512, 1024, "v")
+        plane_turn(2, 1, False)
+        round_out(6, 512, 1024, "v")
         plane_quant(0, 1)
+        plane_turn(4, 1, True)
+        plane_turn(6, 1, False)
         plane_quant(2, 1)
         plane_store_words(1, 0, 4)
-        round_out(6, 512, 1024, "v")
-        plane_turn(4, 1, False)
-        plane_turn(6, 1, True)
         plane_quant(4, 1)
         plane_quant(6, 1)
         plane_store_words(1, 4, 8)
-        plane_store_scales(1)
+        plane_store_scales()

@@ -19,27 +19,17 @@ P = 128
 PACK = 4
 G = N // (P * PACK)
 HALF = 512
-NH = D // HALF
-SUB = 128
-NS = HALF // SUB
-
-MULT_ON_GPSIMD = ()
+CHUNKS = ((0, 512), (512, 768), (768, 1024))
 
 
 def tile_federatednewtonsketchlogistichessian_x1_kernel(tc, x, u, sk, a, b, out, words, scales):
     nc = tc.nc
     with ExitStack() as ctx:
         keep = ctx.enter_context(tc.tile_pool(name="keep", bufs=1))
-        mul_pool = ctx.enter_context(tc.tile_pool(name="mul", bufs=4))
-        grp_pool = ctx.enter_context(tc.tile_pool(name="grp", bufs=4))
-        lr_pool = ctx.enter_context(tc.tile_pool(name="lr", bufs=2))
-        out_pool = ctx.enter_context(tc.tile_pool(name="outp", bufs=6))
-        psum = ctx.enter_context(tc.psum_pool(name="psum", bufs=2))
+        work = ctx.enter_context(tc.tile_pool(name="work", bufs=4))
+        psum = ctx.enter_context(tc.psum_pool(name="psum", bufs=6))
         ctx.enter_context(tc.manual_schedule())
 
-        rows = keep.tile([P, M], BF16, name="rows", align_bytes=64)
-        nc.vector.memset(rows[:], 0.0)
-        nc.sync.dma_start(out=rows[0 : K * G, :], in_=u.rearrange("k (g n) -> (k g) n", g=G))
         x_raw = {}
         sk_raw = {}
 
@@ -58,8 +48,14 @@ def tile_federatednewtonsketchlogistichessian_x1_kernel(tc, x, u, sk, a, b, out,
             )
             sk_raw[k, half] = t
 
+        rows = keep.tile([P, M], BF16, name="rows", align_bytes=64)
+        nc.sync.dma_start(out=rows[0 : K * G, :], in_=u.rearrange("k (g n) -> (k g) n", g=G))
         nc.sync.dma_start(out=rows[4:6, :], in_=a)
         nc.sync.dma_start(out=rows[6:8, :], in_=b)
+        for r in (8, 16):
+            nc.sync.dma_start(out=rows[r : 2 * r, :], in_=a[0:1, :].to_broadcast([r, M]))
+        for r in (32, 64):
+            nc.vector.memset(rows[r : 2 * r, :], 0.0)
         load_x(0, 0, 0)
         load_sk(0, 0)
         load_sk(0, 1)
@@ -75,11 +71,11 @@ def tile_federatednewtonsketchlogistichessian_x1_kernel(tc, x, u, sk, a, b, out,
 
         ident = keep.tile([P, P], F32, name="ident")
         make_identity(nc, ident[:])
-
         warm = keep.tile([P, 1], F32, name="warm")
         nc.vector.memset(warm[:], 0.0)
         warm2 = keep.tile([P, 1], F32, name="warm2")
         nc.scalar.activation(out=warm2[:], in_=warm[:], func=ACT.Exp)
+
         au = keep.tile([P, K * G, PACK], F32, name="au")
         ab_sb = keep.tile([P, 2 * K, PACK], F32, name="ab_sb")
         e1 = keep.tile([P, K * G, PACK], F32, name="e1")
@@ -87,7 +83,6 @@ def tile_federatednewtonsketchlogistichessian_x1_kernel(tc, x, u, sk, a, b, out,
         rec = keep.tile([P, K * G, PACK], F32, name="rec")
         c_sb = keep.tile([P, K * G, PACK], F32, name="c_sb")
         rw = rows[:].bitcast(F32)
-
         row_bank = psum.tile([P, 2, P], F32, name="ut", tag="tr", bufs=2)
         for e in range(2):
             nc.tensor.transpose(row_bank[:, e, :], rw[:, e : M // 2 : 2], ident[:])
@@ -104,7 +99,14 @@ def tile_federatednewtonsketchlogistichessian_x1_kernel(tc, x, u, sk, a, b, out,
         def make_ab():
             nc.vector.tensor_copy(out=ab_sb[:].rearrange("p r (e f) -> p r e f", f=2), in_=u_t[:, 4:8, :, :])
 
+        def copy(engine, dst, src):
+            if engine == "v":
+                nc.vector.tensor_copy(out=dst, in_=src)
+            else:
+                nc.scalar.copy(out=dst, in_=src)
+
         q_mul = {}
+        q_grp = {}
         q_codes = {}
         q_scales = {}
         s_codes = {}
@@ -112,28 +114,21 @@ def tile_federatednewtonsketchlogistichessian_x1_kernel(tc, x, u, sk, a, b, out,
         s_grp = {}
 
         def mult(k, g, h):
-            t = mul_pool.tile([P, PACK, HALF], BF16, name="qm", align_bytes=64)
+            t = work.tile([P, PACK, HALF], BF16, name="qm", align_bytes=64)
             q_mul[k, g, h] = t
             for j in range(PACK):
-                cj = c_sb[:, k * G + g, j : j + 1]
-                if (k, g, h) in MULT_ON_GPSIMD:
-                    nc.gpsimd.tensor_scalar(
-                        out=t[:, j, :], in0=x_raw[k, g, h][:, j, :], scalar1=cj, scalar2=0.0, op0=ALU.mult, op1=ALU.add
-                    )
-                else:
-                    nc.vector.tensor_scalar_mul(out=t[:, j, :], in0=x_raw[k, g, h][:, j, :], scalar1=cj)
+                nc.vector.tensor_scalar_mul(
+                    out=t[:, j, :], in0=x_raw[k, g, h][:, j, :], scalar1=c_sb[:, k * G + g, j : j + 1]
+                )
 
-        q_grp = {}
-
-        def inter(k, g, h, d0=0, d1=HALF, on_vector=False):
+        def inter(k, g, h, engine="s", d0=0, d1=HALF):
             if d0 == 0:
-                q_grp[k, g, h] = grp_pool.tile([P, HALF, PACK], BF16, name="qg", align_bytes=64)
-            dst = q_grp[k, g, h][:, d0:d1, :].rearrange("p (c i) t -> p c t i", i=4)
-            src = q_mul[k, g, h][:, :, d0:d1].rearrange("p t (c i) -> p c t i", i=4)
-            if on_vector:
-                nc.vector.tensor_copy(out=dst, in_=src)
-            else:
-                nc.scalar.copy(out=dst, in_=src)
+                q_grp[k, g, h] = work.tile([P, HALF, PACK], BF16, name="qg", align_bytes=64)
+            copy(
+                engine,
+                q_grp[k, g, h][:, d0:d1, :].rearrange("p (c i) t -> p c t i", i=4),
+                q_mul[k, g, h][:, :, d0:d1].rearrange("p t (c i) -> p c t i", i=4),
+            )
 
         def quant_q(k, g, h, d0=0, d1=HALF):
             if d0 == 0:
@@ -145,21 +140,16 @@ def tile_federatednewtonsketchlogistichessian_x1_kernel(tc, x, u, sk, a, b, out,
                 in_=q_grp[k, g, h][:, d0:d1, :].rearrange("p d t -> p (d t)"),
             )
 
-        def sk_turn(k, half, g, tag, on_vector):
+        def sk_turn(k, half, g, tag, engine="s"):
             if half == 0:
-                s_grp[k, g] = grp_pool.tile([P, M, PACK], BF16, name=f"sg{g}", bufs=2, align_bytes=64)
+                s_grp[k, g] = work.tile([P, M, PACK], BF16, name=f"sg{g}", bufs=2, align_bytes=64)
             xt = psum.tile([P, 2, 2, P], F32, name="xt", tag=tag, bufs=6 if tag == "b" else 2)
             for tt in range(2):
                 w = sk_raw[k, half][:, tt, :].bitcast(F32)
                 for e in range(2):
                     nc.tensor.transpose(xt[:, tt, e, :], w[:, 256 * g + e : 256 * (g + 1) : 2], ident[:])
             dst = s_grp[k, g][:, 256 * half : 256 * half + 256, :].rearrange("p m t -> p (m t)").bitcast(F32)
-            dst = dst.rearrange("p (t m e) -> p t m e", t=2, e=2)
-            src = xt[:].rearrange("p t e m -> p t m e")
-            if on_vector:
-                nc.vector.tensor_copy(out=dst, in_=src)
-            else:
-                nc.scalar.copy(out=dst, in_=src)
+            copy(engine, dst.rearrange("p (t m e) -> p t m e", t=2, e=2), xt[:].rearrange("p t e m -> p t m e"))
 
         def quant_s(k, g):
             codes = keep.tile([P, M], U32, name=f"sc_{k}{g}", align_bytes=64)
@@ -172,10 +162,11 @@ def tile_federatednewtonsketchlogistichessian_x1_kernel(tc, x, u, sk, a, b, out,
 
         y_bank = {}
 
-        def stage1(k, h, s):
-            bank = psum.tile([P, PACK, SUB], F32, name="yb", tag="b", bufs=6)
-            y_bank[k, h, s] = bank
-            cols = slice(SUB * s, SUB * s + SUB)
+        def stage1(k, s):
+            bank = psum.tile([P, PACK, P], F32, name="yb", tag="b", bufs=6)
+            y_bank[k, s] = bank
+            h, lo = divmod(P * s, HALF)
+            cols = slice(lo, lo + P)
             for t in range(PACK):
                 mc = slice(P * t, P * t + P)
                 for g in range(G):
@@ -192,279 +183,278 @@ def tile_federatednewtonsketchlogistichessian_x1_kernel(tc, x, u, sk, a, b, out,
         lr = {}
         lr_codes = {}
         lr_scales = {}
-        for side in range(2):
-            for k in range(K):
-                lr_codes[side, k] = keep.tile([P, D], U32, name=f"lrc_{side}{k}", align_bytes=64)
-                lr_scales[side, k] = keep.tile([P, D], U8, name=f"lrs_{side}{k}", align_bytes=64)
 
-        def weigh(k, h, s, sides=(0, 1), on_scalar=False):
+        def chunk_of(d):
+            for n, (lo, hi) in enumerate(CHUNKS):
+                if lo <= d < hi:
+                    return n, d - lo
+
+        def weigh(k, s, sides=(0, 1), engine="v"):
+            ch, lo = chunk_of(P * s)
+            width = CHUNKS[ch][1] - CHUNKS[ch][0]
+            if (k, ch) not in lr:
+                lr[k, ch] = work.tile([P, 2, width, PACK], BF16, name=f"lr{min(ch, 1)}", bufs=2, align_bytes=64)
+            bank = y_bank[k, s]
             for side in sides:
-                if s == 0 and (side, k, h) not in lr:
-                    lr[side, k, h] = lr_pool.tile([P, HALF, PACK], BF16, name=f"lr{side}", align_bytes=64)
-                dst = lr[side, k, h][:, SUB * s : SUB * s + SUB, :]
                 row = K * side + k
-                if on_scalar:
-                    tmp = lr_pool.tile([P, PACK, SUB], BF16, name="wt", align_bytes=64)
+                half = lr[k, ch][:, side, :, :]
+                dst = half[:, lo : lo + P, :]
+                src = bank[:].rearrange("p t d -> p d t")
+                wt = ab_sb[:, row : row + 1, :].to_broadcast([P, P, PACK])
+                if engine == "s":
+                    tmp = work.tile([P, PACK, P], BF16, name="wt", bufs=2, align_bytes=64)
                     for t in range(PACK):
                         nc.scalar.activation(
-                            out=tmp[:, t, :], in_=y_bank[k, h, s][:, t, :], func=ACT.Copy, scale=ab_sb[:, row, t : t + 1]
+                            out=tmp[:, t, :], in_=bank[:, t, :], func=ACT.Copy, scale=ab_sb[:, row, t : t + 1]
                         )
                     nc.scalar.copy(out=dst, in_=tmp[:].rearrange("p t d -> p d t"))
                 else:
-                    nc.vector.tensor_tensor(
-                        out=dst,
-                        in0=y_bank[k, h, s][:].rearrange("p t d -> p d t"),
-                        in1=ab_sb[:, row : row + 1, :].to_broadcast([P, SUB, PACK]),
-                        op=ALU.mult,
-                    )
+                    nc.vector.tensor_tensor(out=dst, in0=src, in1=wt, op=ALU.mult)
 
-        def quant_lr(side, k, h, s0, s1):
-            cols = slice(HALF * h + SUB * s0, HALF * h + SUB * s1)
+        def quant_lr(k, ch, sides=(0, 1)):
+            width = CHUNKS[ch][1] - CHUNKS[ch][0]
+            if (k, ch) not in lr_codes:
+                lr_codes[k, ch] = keep.tile([P, 2, width], U32, name=f"lrc_{k}{ch}", align_bytes=64)
+                lr_scales[k, ch] = keep.tile([P, 2, width], U8, name=f"lrs_{k}{ch}", align_bytes=64)
+            lo, hi = sides[0], sides[-1] + 1
             nc.vector.quantize_mx(
-                out=lr_codes[side, k][:, cols].bitcast(FP8X4),
-                scales=lr_scales[side, k][:, cols],
-                in_=lr[side, k, h][:, SUB * s0 : SUB * s1, :].rearrange("p d t -> p (d t)"),
+                out=lr_codes[k, ch][:, lo:hi, :].rearrange("p s d -> p (s d)").bitcast(FP8X4),
+                scales=lr_scales[k, ch][:, lo:hi, :].rearrange("p s d -> p (s d)"),
+                in_=lr[k, ch][:, lo:hi, :, :].rearrange("p s d j -> p (s d j)"),
             )
+
+        def left(k, i):
+            ch, lo = chunk_of(P * i)
+            cols = slice(lo, lo + P)
+            return lr_codes[k, ch][:, 0, cols].bitcast(FP8X4), lr_scales[k, ch][:, 0, cols]
+
+        def right(k, ch, cols):
+            return lr_codes[k, ch][:, 1, cols].bitcast(FP8X4), lr_scales[k, ch][:, 1, cols]
+
+        def product(bank, stationary, moving):
+            for k in range(K):
+                w, ws = stationary(k)
+                v, vs = moving(k)
+                nc.tensor.matmul_mx(
+                    out=bank, lhsT=w, lhsT_scale=ws, rhs=v, rhs_scale=vs, start=(k == 0), stop=(k == K - 1)
+                )
 
         o_bank = {}
         o_f32 = {}
         o_bf = {}
 
-        def stage2(i, c0, c1):
-            width = c1 - c0
+        def stage2(i, ch):
+            width = CHUNKS[ch][1] - CHUNKS[ch][0]
             banks = []
-            for ii in range(2):
-                if ii == 0 or width == HALF:
+            for n in range(2):
+                if n == 0 or width == HALF:
                     bank = psum.tile([P, HALF], F32, name="ob", tag="b", bufs=6)
                     banks.append(bank)
-                rows = slice(P * (i + ii), P * (i + ii) + P)
-                lo = 0 if width == HALF else width * ii
-                for k in range(K):
-                    nc.tensor.matmul_mx(
-                        out=bank[:, lo : lo + width],
-                        lhsT=lr_codes[0, k][:, rows].bitcast(FP8X4),
-                        lhsT_scale=lr_scales[0, k][:, rows],
-                        rhs=lr_codes[1, k][:, c0:c1].bitcast(FP8X4),
-                        rhs_scale=lr_scales[1, k][:, c0:c1],
-                        start=(k == 0),
-                        stop=(k == K - 1),
-                    )
-            o_bank[i, c0] = banks
+                lo = 0 if width == HALF else width * n
+                product(
+                    bank[:, lo : lo + width],
+                    lambda k: left(k, i + n),
+                    lambda k: right(k, ch, slice(0, width)),
+                )
+            o_bank[i, ch] = banks
 
-        def emit_out(i, c0, c1, engines="ss", store=True):
-            f = c0 // HALF
+        def emit_out(i, ch, engines="ss"):
+            f = min(ch, 1)
             if (i, f) not in o_f32:
-                o_f32[i, f] = out_pool.tile([P, 2, HALF], F32, name="o32", bufs=8, align_bytes=64)
-                o_bf[i, f] = out_pool.tile([P, 2, 2, P, 2], BF16, name="o16", bufs=8, align_bytes=64)
-            lo, hi = c0 - HALF * f, c1 - HALF * f
-            banks = o_bank[i, c0]
-            for n, bank in enumerate(banks):
-                if len(banks) == 2:
-                    dst, src = o_f32[i, f][:, n, lo:hi], bank[:]
-                else:
-                    dst, src = o_f32[i, f][:, :, lo:hi], bank[:].rearrange("p (i c) -> p i c", i=2)
-                if engines[n] == "v":
-                    nc.vector.tensor_copy(out=dst, in_=src)
-                else:
-                    nc.scalar.copy(out=dst, in_=src)
-            if store:
-                store_out(i, c0, c1)
+                o_f32[i, f] = work.tile([P, 2, HALF], F32, name="o32", bufs=8, align_bytes=64)
+            banks = o_bank[i, ch]
+            if ch == 0:
+                for n in range(2):
+                    copy(engines[n], o_f32[i, f][:, n, :], banks[n][:])
+            else:
+                lo, hi = CHUNKS[ch][0] - HALF, CHUNKS[ch][1] - HALF
+                copy(engines[0], o_f32[i, f][:, :, lo:hi], banks[0][:].rearrange("p (i c) -> p i c", i=2))
 
         def store_out(i, c0, c1):
             f = c0 // HALF
-            lo, hi = c0 - HALF * f, c1 - HALF * f
             nc.sync.dma_start(
-                out=out[P * i : P * i + 2 * P, c0:c1].rearrange("(i p) c -> p i c", i=2), in_=o_f32[i, f][:, :, lo:hi]
+                out=out[P * i : P * i + 2 * P, c0:c1].rearrange("(i p) c -> p i c", i=2),
+                in_=o_f32[i, f][:, :, c0 - HALF * f : c1 - HALF * f],
             )
 
-        def round_out(i, c0, c1, eng):
-            f = c0 // HALF
-            lo, hi = c0 - HALF * f, c1 - HALF * f
-            for ii in range(2):
-                dst = o_bf[i, f][:, ii, :, lo // 4 : hi // 4, :]
-                if eng == "s":
-                    banks = o_bank[i, c0]
-                    src = banks[ii][:] if len(banks) == 2 else banks[0][:, (hi - lo) * ii : (hi - lo) * (ii + 1)]
-                    nc.scalar.copy(out=dst, in_=src.rearrange("p (m u e) -> p u m e", u=2, e=2))
-                else:
-                    src = o_f32[i, f][:, ii, lo:hi].rearrange("p (m u e) -> p u m e", u=2, e=2)
-                    nc.vector.tensor_copy(out=dst, in_=src)
+        def round_out(i, f, lo=0, hi=HALF, engine="v"):
+            if (i, f) not in o_bf:
+                o_bf[i, f] = work.tile([P, 2, 2, P, 2], BF16, name="o16", bufs=6, align_bytes=64)
+            for n in range(2):
+                src = o_bank[i, 0][n][:] if engine == "s" else o_f32[i, f][:, n, lo:hi]
+                copy(engine, o_bf[i, f][:, n, :, lo // 4 : hi // 4, :], src.rearrange("p (m u e) -> p u m e", u=2, e=2))
 
         pl_codes = {}
-        pl_scales = {}
-        for f in range(NH):
+        for f in range(2):
             pl_codes[f] = keep.tile([P, D], U32, name=f"plc_{f}", align_bytes=64)
-        pl_scale_tile = keep.tile([P, NH, D], U8, name="pls", align_bytes=64)
-        for f in range(NH):
-            pl_scales[f] = pl_scale_tile[:, f, :]
-
+        pl_scales = keep.tile([P, 2, D], U8, name="pls", align_bytes=64)
         pl_grp = {}
 
-        def plane_turn(i, f, on_vector):
-            xt = psum.tile([P, 2, 2, P], F32, name="pt", tag="tr")
-            for ii in range(2):
+        def plane_turn(i, f, engine):
+            xt = psum.tile([P, 2, 2, P], F32, name="pt", tag="tr", bufs=2)
+            for n in range(2):
                 for e in range(2):
-                    w = o_bf[i, f][:, ii, e, :, :].rearrange("p m e -> p (m e)").bitcast(F32)
-                    nc.tensor.transpose(xt[:, ii, e, :], w, ident[:])
-            grp = out_pool.tile([P, 2 * P, PACK], BF16, name="pg", bufs=4, align_bytes=64)
+                    w = o_bf[i, f][:, n, e, :, :].rearrange("p m e -> p (m e)").bitcast(F32)
+                    nc.tensor.transpose(xt[:, n, e, :], w, ident[:])
+            grp = work.tile([P, 2 * P, PACK], BF16, name="pg", bufs=4, align_bytes=64)
             pl_grp[i, f] = grp
             dst = grp[:].rearrange("p d t -> p (d t)").bitcast(F32).rearrange("p (i d e) -> p i d e", i=2, e=2)
-            src = xt[:].rearrange("p i e d -> p i d e")
-            if on_vector:
-                nc.vector.tensor_copy(out=dst, in_=src)
-            else:
-                nc.scalar.copy(out=dst, in_=src)
+            copy(engine, dst, xt[:].rearrange("p i e d -> p i d e"))
 
         def plane_quant(i, f):
             cols = slice(P * i, P * i + 2 * P)
             nc.vector.quantize_mx(
                 out=pl_codes[f][:, cols].bitcast(FP8X4),
-                scales=pl_scales[f][:, cols],
+                scales=pl_scales[:, f, cols],
                 in_=pl_grp[i, f][:].rearrange("p d t -> p (d t)"),
             )
 
-        def plane_store_words(f, i0, i1):
+        def store_words(f, i0, i1):
             nc.sync.dma_start(
                 out=words[f, :, P * i0 : P * i1, :].rearrange("p d t -> p (d t)").bitcast(I32),
                 in_=pl_codes[f][:, P * i0 : P * i1].bitcast(I32),
             )
 
-        def plane_store_scales():
+        def store_scales():
             for q in range(4):
                 nc.sync.dma_start(
                     out=scales[:, 4 * q : 4 * q + 4, :].bitcast(I32).rearrange("f r m -> r f m"),
-                    in_=pl_scale_tile[32 * q : 32 * q + 4, :, :].bitcast(I32),
+                    in_=pl_scales[32 * q : 32 * q + 4, :, :].bitcast(I32),
                 )
 
         mult(0, 0, 0)
         make_ab()
-        sk_turn(0, 0, 0, "b", False)
-        sk_turn(0, 0, 1, "b", False)
-        inter(0, 0, 0, 0, 512, True)
-        sk_turn(0, 1, 0, "b", False)
-        sk_turn(0, 1, 1, "b", False)
+        sk_turn(0, 0, 0, "b")
+        sk_turn(0, 0, 1, "b")
+        inter(0, 0, 0, "v")
+        sk_turn(0, 1, 0, "b")
+        sk_turn(0, 1, 1, "b")
         quant_q(0, 0, 0)
         mult(0, 1, 0)
         quant_s(0, 0)
-        inter(0, 1, 0, 0, 256, True)
-        inter(0, 1, 0, 256, 512)
+        inter(0, 1, 0, "v", 0, 256)
+        inter(0, 1, 0, "s", 256, 512)
         quant_s(0, 1)
         quant_q(0, 1, 0, 0, 256)
         mult(1, 0, 0)
         quant_q(0, 1, 0, 256, 512)
         inter(1, 0, 0)
-        for s in range(NS):
-            stage1(0, 0, s)
-        sk_turn(1, 0, 0, "tr", False)
-        sk_turn(1, 0, 1, "tr", False)
-        weigh(0, 0, 0)
-        weigh(0, 0, 1)
+        for s in range(4):
+            stage1(0, s)
+        sk_turn(1, 0, 0, "tr")
+        sk_turn(1, 0, 1, "tr")
+        weigh(0, 0)
+        weigh(0, 1)
         mult(1, 1, 0)
-        weigh(0, 0, 2)
-        weigh(0, 0, 3)
-        sk_turn(1, 1, 0, "b", False)
-        sk_turn(1, 1, 1, "b", False)
+        weigh(0, 2)
+        weigh(0, 3)
+        sk_turn(1, 1, 0, "b")
+        sk_turn(1, 1, 1, "b")
         inter(1, 1, 0)
-        quant_lr(0, 0, 0, 0, 4)
-        quant_lr(1, 0, 0, 0, 4)
         quant_q(1, 0, 0)
-        quant_s(1, 0)
         mult(0, 0, 1)
+        quant_s(1, 0)
         quant_s(1, 1)
         quant_q(1, 1, 0)
-        mult(0, 1, 1)
-        for s in range(NS):
-            stage1(1, 0, s)
+        for s in range(4):
+            stage1(1, s)
         inter(0, 0, 1)
+        quant_lr(0, 0)
+        mult(0, 1, 1)
         inter(0, 1, 1)
-        weigh(1, 0, 0)
-        weigh(1, 0, 1)
+        weigh(1, 0)
+        weigh(1, 1)
         mult(1, 0, 1)
         quant_q(0, 0, 1)
-        weigh(1, 0, 2)
+        weigh(1, 2)
         mult(1, 1, 1)
         quant_q(0, 1, 1)
-        stage1(0, 1, 0)
-        stage1(0, 1, 1)
-        weigh(1, 0, 3)
+        stage1(0, 4)
+        stage1(0, 5)
+        weigh(1, 3)
         inter(1, 0, 1)
         inter(1, 1, 1)
-        quant_lr(0, 1, 0, 0, 4)
-        quant_lr(1, 1, 0, 0, 4)
-        weigh(0, 1, 0)
-        weigh(0, 1, 1)
+        weigh(0, 4, (0,))
+        quant_lr(1, 0)
+        weigh(0, 4, (1,))
+        weigh(0, 5)
         quant_q(1, 0, 1)
         for i in (0, 2):
-            stage2(i, 0, 512)
-            emit_out(i, 0, 512)
-            round_out(i, 0, 512, "s")
-        quant_lr(0, 0, 1, 0, 2)
-        quant_lr(1, 0, 1, 0, 2)
+            stage2(i, 0)
+            emit_out(i, 0)
+            store_out(i, 0, 512)
+            round_out(i, 0, engine="s")
+        stage1(0, 6)
+        quant_lr(0, 1)
         quant_q(1, 1, 1)
-        stage1(0, 1, 2)
-        stage1(0, 1, 3)
-        weigh(0, 1, 2)
-        stage1(1, 1, 0)
-        stage1(1, 1, 1)
-        weigh(1, 1, 0)
-        weigh(1, 1, 1)
-        plane_turn(0, 0, False)
-        plane_turn(2, 0, False)
-        quant_lr(0, 1, 1, 0, 2)
-        quant_lr(1, 1, 1, 0, 2)
-        stage1(1, 1, 2)
-        weigh(0, 1, 3)
-        stage2(4, 0, 512)
-        emit_out(4, 0, 512)
-        stage2(0, 512, 768)
-        emit_out(0, 512, 768)
-        stage1(1, 1, 3)
-        quant_lr(0, 0, 1, 2, 4)
-        quant_lr(1, 0, 1, 2, 4)
-        weigh(1, 1, 2, (0,))
-        weigh(1, 1, 3, (0,))
+        weigh(0, 6)
+        stage1(1, 4)
+        stage1(1, 5)
+        stage1(0, 7)
+        plane_turn(0, 0, "s")
+        weigh(1, 4)
+        weigh(1, 5)
+        quant_lr(1, 1)
+        plane_turn(2, 0, "s")
+        weigh(0, 7)
+        stage1(1, 6)
+        stage2(4, 0)
+        emit_out(4, 0)
+        store_out(4, 0, 512)
+        round_out(4, 0, engine="s")
+        stage2(0, 1)
+        emit_out(0, 1)
+        store_out(0, 512, 768)
+        stage1(1, 7)
+        weigh(1, 6, (0,))
+        quant_lr(0, 2)
+        weigh(1, 7, (0,))
         for i in (2, 4):
-            stage2(i, 512, 768)
-            emit_out(i, 512, 768)
+            stage2(i, 1)
+            emit_out(i, 1)
+            store_out(i, 512, 768)
+        plane_turn(4, 0, "s")
         plane_quant(0, 0)
-        quant_lr(0, 1, 1, 2, 4)
-        weigh(1, 1, 2, (1,))
-        weigh(1, 1, 3, (1,))
+        quant_lr(1, 2, (0,))
+        weigh(1, 6, (1,))
+        weigh(1, 7, (1,))
+        stage2(6, 0)
+        stage2(6, 1)
+        emit_out(6, 0)
+        store_out(6, 0, 512)
+        emit_out(6, 1)
         plane_quant(2, 0)
-        plane_store_words(0, 0, 4)
-        stage2(6, 0, 512)
-        emit_out(6, 0, 512)
-        stage2(6, 512, 768)
-        emit_out(6, 512, 768, store=False)
-        quant_lr(1, 1, 1, 2, 4)
-        round_out(4, 0, 512, "v")
-        stage2(0, 768, 1024)
-        stage2(2, 768, 1024)
-        emit_out(0, 768, 1024)
-        round_out(6, 0, 512, "v")
-        plane_turn(4, 0, True)
-        emit_out(2, 768, 1024)
-        stage2(4, 768, 1024)
-        round_out(0, 512, 1024, "v")
-        emit_out(4, 768, 1024)
-        plane_turn(6, 0, True)
-        stage2(6, 768, 1024)
-        round_out(2, 512, 1024, "v")
+        store_words(0, 0, 4)
+        quant_lr(1, 2, (1,))
+        stage2(0, 2)
+        round_out(6, 0)
         plane_quant(4, 0)
-        plane_turn(0, 1, False)
-        emit_out(6, 768, 1024, store=False)
+        emit_out(0, 2)
+        store_out(0, 768, 1024)
+        stage2(2, 2)
+        emit_out(2, 2)
+        store_out(2, 768, 1024)
+        stage2(4, 2)
+        round_out(0, 1)
+        plane_turn(6, 0, "v")
+        emit_out(4, 2)
+        store_out(4, 768, 1024)
+        stage2(6, 2)
+        round_out(2, 1)
+        plane_turn(0, 1, "s")
+        emit_out(6, 2)
         store_out(6, 512, 1024)
         plane_quant(6, 0)
-        plane_store_words(0, 4, 8)
-        round_out(4, 512, 1024, "v")
-        plane_turn(2, 1, False)
-        round_out(6, 512, 1024, "v")
+        store_words(0, 4, 8)
+        round_out(4, 1)
+        plane_turn(2, 1, "s")
+        round_out(6, 1)
         plane_quant(0, 1)
-        plane_turn(4, 1, True)
-        plane_turn(6, 1, False)
+        plane_turn(4, 1, "v")
+        plane_turn(6, 1, "s")
         plane_quant(2, 1)
-        plane_store_words(1, 0, 4)
+        store_words(1, 0, 4)
         plane_quant(4, 1)
         plane_quant(6, 1)
-        plane_store_words(1, 4, 8)
-        plane_store_scales()
+        store_words(1, 4, 8)
+        store_scales()

@@ -113,13 +113,16 @@ def tile_federatednewtonsketchlogistichessian_x1_kernel(tc, x, u, sk, a, b, out,
         s_scales = {}
         s_grp = {}
 
-        def mult(k, g, h):
+        def mult(k, g, h, engines="vvvv"):
             t = work.tile([P, PACK, HALF], BF16, name="qm", align_bytes=64)
             q_mul[k, g, h] = t
             for j in range(PACK):
-                nc.vector.tensor_scalar_mul(
-                    out=t[:, j, :], in0=x_raw[k, g, h][:, j, :], scalar1=c_sb[:, k * G + g, j : j + 1]
-                )
+                src = x_raw[k, g, h][:, j, :]
+                cj = c_sb[:, k * G + g, j : j + 1]
+                if engines[j] == "v":
+                    nc.vector.tensor_scalar_mul(out=t[:, j, :], in0=src, scalar1=cj)
+                else:
+                    nc.scalar.activation(out=t[:, j, :], in_=src, func=ACT.Copy, scale=cj)
 
         def inter(k, g, h, engine="s", d0=0, d1=HALF):
             if d0 == 0:
@@ -261,28 +264,34 @@ def tile_federatednewtonsketchlogistichessian_x1_kernel(tc, x, u, sk, a, b, out,
         def emit_out(i, ch, engines="ss"):
             f = min(ch, 1)
             if (i, f) not in o_f32:
-                o_f32[i, f] = work.tile([P, 2, HALF], F32, name="o32", bufs=8, align_bytes=64)
+                shape = [P, 2, HALF] if f == 0 else [P, 2, 2, HALF // 2]
+                o_f32[i, f] = work.tile(shape, F32, name="o32", bufs=8, align_bytes=64)
             banks = o_bank[i, ch]
             if ch == 0:
                 for n in range(2):
                     copy(engines[n], o_f32[i, f][:, n, :], banks[n][:])
             else:
-                lo, hi = CHUNKS[ch][0] - HALF, CHUNKS[ch][1] - HALF
-                copy(engines[0], o_f32[i, f][:, :, lo:hi], banks[0][:].rearrange("p (i c) -> p i c", i=2))
+                copy(engines[0], o_f32[i, f][:, ch - 1, :, :], banks[0][:].rearrange("p (i c) -> p i c", i=2))
 
-        def store_out(i, c0, c1):
-            f = c0 // HALF
-            nc.sync.dma_start(
-                out=out[P * i : P * i + 2 * P, c0:c1].rearrange("(i p) c -> p i c", i=2),
-                in_=o_f32[i, f][:, :, c0 - HALF * f : c1 - HALF * f],
-            )
+        def store_out(i, ch):
+            c0, c1 = CHUNKS[ch]
+            src = o_f32[i, 0][:] if ch == 0 else o_f32[i, 1][:, ch - 1, :, :]
+            nc.sync.dma_start(out=out[P * i : P * i + 2 * P, c0:c1].rearrange("(i p) c -> p i c", i=2), in_=src)
 
-        def round_out(i, f, lo=0, hi=HALF, engine="v"):
-            if (i, f) not in o_bf:
-                o_bf[i, f] = work.tile([P, 2, 2, P, 2], BF16, name="o16", bufs=6, align_bytes=64)
+        def round_out(i, f, engine="v"):
+            o_bf[i, f] = work.tile([P, 2, 2, P, 2], BF16, name="o16", bufs=6, align_bytes=64)
             for n in range(2):
-                src = o_bank[i, 0][n][:] if engine == "s" else o_f32[i, f][:, n, lo:hi]
-                copy(engine, o_bf[i, f][:, n, :, lo // 4 : hi // 4, :], src.rearrange("p (m u e) -> p u m e", u=2, e=2))
+                dst = o_bf[i, f][:, n, :, :, :]
+                if f == 0:
+                    src = o_bank[i, 0][n][:] if engine == "s" else o_f32[i, f][:, n, :]
+                    copy(engine, dst, src.rearrange("p (m u e) -> p u m e", u=2, e=2))
+                else:
+                    src = o_f32[i, f][:, :, n, :]
+                    copy(
+                        engine,
+                        dst.rearrange("p u (q m) e -> p u q m e", q=2),
+                        src.rearrange("p q (m u e) -> p u q m e", u=2, e=2),
+                    )
 
         pl_codes = {}
         for f in range(2):
@@ -331,11 +340,11 @@ def tile_federatednewtonsketchlogistichessian_x1_kernel(tc, x, u, sk, a, b, out,
         sk_turn(0, 1, 1, "b")
         quant_q(0, 0, 0)
         mult(0, 1, 0)
-        quant_s(0, 0)
         inter(0, 1, 0, "v", 0, 256)
         inter(0, 1, 0, "s", 256, 512)
-        quant_s(0, 1)
+        quant_s(0, 0)
         quant_q(0, 1, 0, 0, 256)
+        quant_s(0, 1)
         mult(1, 0, 0)
         quant_q(0, 1, 0, 256, 512)
         inter(1, 0, 0)
@@ -367,12 +376,12 @@ def tile_federatednewtonsketchlogistichessian_x1_kernel(tc, x, u, sk, a, b, out,
         mult(1, 0, 1)
         quant_q(0, 0, 1)
         weigh(1, 2)
-        mult(1, 1, 1)
         quant_q(0, 1, 1)
         stage1(0, 4)
         stage1(0, 5)
         weigh(1, 3)
         inter(1, 0, 1)
+        mult(1, 1, 1, "vvss")
         inter(1, 1, 1)
         weigh(0, 4, (0,))
         quant_lr(1, 0)
@@ -382,7 +391,7 @@ def tile_federatednewtonsketchlogistichessian_x1_kernel(tc, x, u, sk, a, b, out,
         for i in (0, 2):
             stage2(i, 0)
             emit_out(i, 0)
-            store_out(i, 0, 512)
+            store_out(i, 0)
             round_out(i, 0, engine="s")
         stage1(0, 6)
         quant_lr(0, 1)
@@ -400,11 +409,11 @@ def tile_federatednewtonsketchlogistichessian_x1_kernel(tc, x, u, sk, a, b, out,
         stage1(1, 6)
         stage2(4, 0)
         emit_out(4, 0)
-        store_out(4, 0, 512)
+        store_out(4, 0)
         round_out(4, 0, engine="s")
         stage2(0, 1)
         emit_out(0, 1)
-        store_out(0, 512, 768)
+        store_out(0, 1)
         stage1(1, 7)
         weigh(1, 6, (0,))
         quant_lr(0, 2)
@@ -412,7 +421,7 @@ def tile_federatednewtonsketchlogistichessian_x1_kernel(tc, x, u, sk, a, b, out,
         for i in (2, 4):
             stage2(i, 1)
             emit_out(i, 1)
-            store_out(i, 512, 768)
+            store_out(i, 1)
         plane_turn(4, 0, "s")
         plane_quant(0, 0)
         quant_lr(1, 2, (0,))
@@ -420,37 +429,38 @@ def tile_federatednewtonsketchlogistichessian_x1_kernel(tc, x, u, sk, a, b, out,
         weigh(1, 7, (1,))
         stage2(6, 0)
         stage2(6, 1)
-        emit_out(6, 0)
-        store_out(6, 0, 512)
-        emit_out(6, 1)
         plane_quant(2, 0)
         store_words(0, 0, 4)
         quant_lr(1, 2, (1,))
+        emit_out(6, 0)
+        store_out(6, 0)
+        emit_out(6, 1)
+        store_out(6, 1)
         stage2(0, 2)
         round_out(6, 0)
         plane_quant(4, 0)
         emit_out(0, 2)
-        store_out(0, 768, 1024)
+        store_out(0, 2)
         stage2(2, 2)
         emit_out(2, 2)
-        store_out(2, 768, 1024)
+        store_out(2, 2)
         stage2(4, 2)
         round_out(0, 1)
         plane_turn(6, 0, "v")
         emit_out(4, 2)
-        store_out(4, 768, 1024)
+        store_out(4, 2)
         stage2(6, 2)
         round_out(2, 1)
-        plane_turn(0, 1, "s")
         emit_out(6, 2)
-        store_out(6, 512, 1024)
+        store_out(6, 2)
+        plane_turn(0, 1, "s")
         plane_quant(6, 0)
         store_words(0, 4, 8)
         round_out(4, 1)
         plane_turn(2, 1, "s")
         round_out(6, 1)
         plane_quant(0, 1)
-        plane_turn(4, 1, "v")
+        plane_turn(4, 1, "s")
         plane_turn(6, 1, "s")
         plane_quant(2, 1)
         store_words(1, 0, 4)

from contextlib import ExitStack

import concourse.mybir as mybir
from concourse.masks import make_identity

K, M, N, D = 2, 512, 1024, 1024
FLOPS = 2 * K * M * N * D + 2 * K * M * D * D

F32 = mybir.dt.float32
BF16 = mybir.dt.bfloat16
U32 = mybir.dt.uint32
I32 = mybir.dt.int32
U8 = mybir.dt.uint8
FP8X4 = mybir.dt.float8_e4m3fn_x4
ACT = mybir.ActivationFunctionType
ALU = mybir.AluOpType

P = 128
PACK = 4
G = N // (P * PACK)
HALF = 512
CHUNKS = ((0, 512), (512, 768), (768, 1024))


def tile_federatednewtonsketchlogistichessian_x1_kernel(tc, x, u, sk, a, b, out, words, scales):
    nc = tc.nc
    with ExitStack() as ctx:
        keep = ctx.enter_context(tc.tile_pool(name="keep", bufs=1))
        work = ctx.enter_context(tc.tile_pool(name="work", bufs=4))
        psum = ctx.enter_context(tc.psum_pool(name="psum", bufs=6))
        ctx.enter_context(tc.manual_schedule())

        x_raw = {}
        sk_raw = {}

        def load_x(k, g, h):
            t = keep.tile([P, PACK, HALF], BF16, name=f"x_{k}{g}{h}", align_bytes=64)
            nc.sync.dma_start(
                out=t[:],
                in_=x[k, 512 * g : 512 * g + 512, HALF * h : HALF * h + HALF].rearrange("(p j) d -> p j d", j=PACK),
            )
            x_raw[k, g, h] = t

        def load_sk(k, half):
            t = keep.tile([P, 2, N], BF16, name=f"sk_{k}{half}", align_bytes=64)
            nc.sync.dma_start(
                out=t[:], in_=sk[k].rearrange("(m t) n -> m t n", t=PACK)[:, 2 * half : 2 * half + 2, :]
            )
            sk_raw[k, half] = t

        rows = keep.tile([P, M], BF16, name="rows", align_bytes=64)
        nc.sync.dma_start(out=rows[0 : K * G, :], in_=u.rearrange("k (g n) -> (k g) n", g=G))
        nc.sync.dma_start(out=rows[4:6, :], in_=a)
        nc.sync.dma_start(out=rows[6:8, :], in_=b)
        for r in (8, 16):
            nc.sync.dma_start(out=rows[r : 2 * r, :], in_=a[0:1, :].to_broadcast([r, M]))
        for r in (32, 64):
            nc.vector.memset(rows[r : 2 * r, :], 0.0)
        load_x(0, 0, 0)
        load_sk(0, 0)
        load_sk(0, 1)
        load_x(0, 1, 0)
        load_x(1, 0, 0)
        load_x(1, 1, 0)
        load_sk(1, 0)
        load_sk(1, 1)
        load_x(0, 0, 1)
        load_x(0, 1, 1)
        load_x(1, 0, 1)
        load_x(1, 1, 1)

        ident = keep.tile([P, P], F32, name="ident")
        make_identity(nc, ident[:])
        warm = keep.tile([P, 1], F32, name="warm")
        nc.vector.memset(warm[:], 0.0)
        warm2 = keep.tile([P, 1], F32, name="warm2")
        nc.scalar.activation(out=warm2[:], in_=warm[:], func=ACT.Exp)

        au = keep.tile([P, K * G, PACK], F32, name="au")
        ab_sb = keep.tile([P, 2 * K, PACK], F32, name="ab_sb")
        e1 = keep.tile([P, K * G, PACK], F32, name="e1")
        e2 = keep.tile([P, K * G, PACK], F32, name="e2")
        rec = keep.tile([P, K * G, PACK], F32, name="rec")
        c_sb = keep.tile([P, K * G, PACK], F32, name="c_sb")
        rw = rows[:].bitcast(F32)
        row_bank = psum.tile([P, 2, P], F32, name="ut", tag="tr", bufs=2)
        for e in range(2):
            nc.tensor.transpose(row_bank[:, e, :], rw[:, e : M // 2 : 2], ident[:])
        u_t = row_bank[:].bitcast(BF16).rearrange("p e (r f) -> p r e f", f=2)
        nc.scalar.activation(
            out=au[:].rearrange("p r (e f) -> p r e f", f=2), in_=u_t[:, 0:4, :, :], func=ACT.Abs
        )
        nc.scalar.activation(out=e2[:], in_=au[:], func=ACT.Exp, scale=-1.0)
        nc.scalar.activation(out=e1[:], in_=au[:], func=ACT.Exp, scale=-0.5)
        nc.vector.tensor_scalar_add(out=e2[:], in0=e2[:], scalar1=1.0)
        nc.vector.reciprocal(out=rec[:], in_=e2[:])
        nc.vector.tensor_tensor(out=c_sb[:], in0=rec[:], in1=e1[:], op=ALU.mult)

        def make_ab():
            nc.vector.tensor_copy(out=ab_sb[:].rearrange("p r (e f) -> p r e f", f=2), in_=u_t[:, 4:8, :, :])

        def copy(engine, dst, src):
            if engine == "v":
                nc.vector.tensor_copy(out=dst, in_=src)
            else:
                nc.scalar.copy(out=dst, in_=src)

        q_mul = {}
        q_grp = {}
        q_codes = {}
        q_scales = {}
        s_codes = {}
        s_scales = {}
        s_grp = {}

        def mult(k, g, h, engines="vvvv"):
            t = work.tile([P, PACK, HALF], BF16, name="qm", align_bytes=64)
            q_mul[k, g, h] = t
            for j in range(PACK):
                src = x_raw[k, g, h][:, j, :]
                cj = c_sb[:, k * G + g, j : j + 1]
                if engines[j] == "v":
                    nc.vector.tensor_scalar_mul(out=t[:, j, :], in0=src, scalar1=cj)
                else:
                    nc.scalar.activation(out=t[:, j, :], in_=src, func=ACT.Copy, scale=cj)

        def inter(k, g, h, engine="s", d0=0, d1=HALF):
            if d0 == 0:
                q_grp[k, g, h] = work.tile([P, HALF, PACK], BF16, name="qg", align_bytes=64)
            copy(
                engine,
                q_grp[k, g, h][:, d0:d1, :].rearrange("p (c i) t -> p c t i", i=4),
                q_mul[k, g, h][:, :, d0:d1].rearrange("p t (c i) -> p c t i", i=4),
            )

        def quant_q(k, g, h, d0=0, d1=HALF):
            if d0 == 0:
                q_codes[k, g, h] = keep.tile([P, HALF], U32, name=f"qc_{k}{g}{h}", align_bytes=64)
                q_scales[k, g, h] = keep.tile([P, HALF], U8, name=f"qs_{k}{g}{h}", align_bytes=64)
            nc.vector.quantize_mx(
                out=q_codes[k, g, h][:, d0:d1].bitcast(FP8X4),
                scales=q_scales[k, g, h][:, d0:d1],
                in_=q_grp[k, g, h][:, d0:d1, :].rearrange("p d t -> p (d t)"),
            )

        def sk_turn(k, half, g, tag, engine="s"):
            if half == 0:
                s_grp[k, g] = work.tile([P, M, PACK], BF16, name=f"sg{g}", bufs=2, align_bytes=64)
            xt = psum.tile([P, 2, 2, P], F32, name="xt", tag=tag, bufs=6 if tag == "b" else 2)
            for tt in range(2):
                w = sk_raw[k, half][:, tt, :].bitcast(F32)
                for e in range(2):
                    nc.tensor.transpose(xt[:, tt, e, :], w[:, 256 * g + e : 256 * (g + 1) : 2], ident[:])
            dst = s_grp[k, g][:, 256 * half : 256 * half + 256, :].rearrange("p m t -> p (m t)").bitcast(F32)
            copy(engine, dst.rearrange("p (t m e) -> p t m e", t=2, e=2), xt[:].rearrange("p t e m -> p t m e"))

        def quant_s(k, g):
            codes = keep.tile([P, M], U32, name=f"sc_{k}{g}", align_bytes=64)
            sc = keep.tile([P, M], U8, name=f"ss_{k}{g}", align_bytes=64)
            nc.vector.quantize_mx(
                out=codes[:].bitcast(FP8X4), scales=sc[:], in_=s_grp[k, g][:].rearrange("p m t -> p (m t)")
            )
            s_codes[k, g] = codes
            s_scales[k, g] = sc

        y_bank = {}

        def stage1(k, s):
            bank = psum.tile([P, PACK, P], F32, name="yb", tag="b", bufs=6)
            y_bank[k, s] = bank
            h, lo = divmod(P * s, HALF)
            cols = slice(lo, lo + P)
            for t in range(PACK):
                mc = slice(P * t, P * t + P)
                for g in range(G):
                    nc.tensor.matmul_mx(
                        out=bank[:, t, :],
                        lhsT=s_codes[k, g][:, mc].bitcast(FP8X4),
                        lhsT_scale=s_scales[k, g][:, mc],
                        rhs=q_codes[k, g, h][:, cols].bitcast(FP8X4),
                        rhs_scale=q_scales[k, g, h][:, cols],
                        start=(g == 0),
                        stop=(g == G - 1),
                    )

        lr = {}
        lr_codes = {}
        lr_scales = {}

        def chunk_of(d):
            for n, (lo, hi) in enumerate(CHUNKS):
                if lo <= d < hi:
                    return n, d - lo

        def weigh(k, s, sides=(0, 1), engine="v"):
            ch, lo = chunk_of(P * s)
            width = CHUNKS[ch][1] - CHUNKS[ch][0]
            if (k, ch) not in lr:
                lr[k, ch] = work.tile([P, 2, width, PACK], BF16, name=f"lr{min(ch, 1)}", bufs=2, align_bytes=64)
            bank = y_bank[k, s]
            for side in sides:
                row = K * side + k
                half = lr[k, ch][:, side, :, :]
                dst = half[:, lo : lo + P, :]
                src = bank[:].rearrange("p t d -> p d t")
                wt = ab_sb[:, row : row + 1, :].to_broadcast([P, P, PACK])
                if engine == "s":
                    tmp = work.tile([P, PACK, P], BF16, name="wt", bufs=2, align_bytes=64)
                    for t in range(PACK):
                        nc.scalar.activation(
                            out=tmp[:, t, :], in_=bank[:, t, :], func=ACT.Copy, scale=ab_sb[:, row, t : t + 1]
                        )
                    nc.scalar.copy(out=dst, in_=tmp[:].rearrange("p t d -> p d t"))
                else:
                    nc.vector.tensor_tensor(out=dst, in0=src, in1=wt, op=ALU.mult)

        def quant_lr(k, ch, sides=(0, 1)):
            width = CHUNKS[ch][1] - CHUNKS[ch][0]
            if (k, ch) not in lr_codes:
                lr_codes[k, ch] = keep.tile([P, 2, width], U32, name=f"lrc_{k}{ch}", align_bytes=64)
                lr_scales[k, ch] = keep.tile([P, 2, width], U8, name=f"lrs_{k}{ch}", align_bytes=64)
            lo, hi = sides[0], sides[-1] + 1
            nc.vector.quantize_mx(
                out=lr_codes[k, ch][:, lo:hi, :].rearrange("p s d -> p (s d)").bitcast(FP8X4),
                scales=lr_scales[k, ch][:, lo:hi, :].rearrange("p s d -> p (s d)"),
                in_=lr[k, ch][:, lo:hi, :, :].rearrange("p s d j -> p (s d j)"),
            )

        def left(k, i):
            ch, lo = chunk_of(P * i)
            cols = slice(lo, lo + P)
            return lr_codes[k, ch][:, 0, cols].bitcast(FP8X4), lr_scales[k, ch][:, 0, cols]

        def right(k, ch, cols):
            return lr_codes[k, ch][:, 1, cols].bitcast(FP8X4), lr_scales[k, ch][:, 1, cols]

        def product(bank, stationary, moving):
            for k in range(K):
                w, ws = stationary(k)
                v, vs = moving(k)
                nc.tensor.matmul_mx(
                    out=bank, lhsT=w, lhsT_scale=ws, rhs=v, rhs_scale=vs, start=(k == 0), stop=(k == K - 1)
                )

        o_bank = {}
        o_f32 = {}
        o_bf = {}

        def stage2(i, ch):
            width = CHUNKS[ch][1] - CHUNKS[ch][0]
            banks = []
            for n in range(2):
                if n == 0 or width == HALF:
                    bank = psum.tile([P, HALF], F32, name="ob", tag="b", bufs=6)
                    banks.append(bank)
                lo = 0 if width == HALF else width * n
                product(
                    bank[:, lo : lo + width],
                    lambda k: left(k, i + n),
                    lambda k: right(k, ch, slice(0, width)),
                )
            o_bank[i, ch] = banks

        def emit_out(i, ch, engines="ss"):
            f = min(ch, 1)
            if (i, f) not in o_f32:
                shape = [P, 2, HALF] if f == 0 else [P, 2, 2, HALF // 2]
                o_f32[i, f] = work.tile(shape, F32, name="o32", bufs=8, align_bytes=64)
            banks = o_bank[i, ch]
            if ch == 0:
                for n in range(2):
                    copy(engines[n], o_f32[i, f][:, n, :], banks[n][:])
            else:
                copy(engines[0], o_f32[i, f][:, ch - 1, :, :], banks[0][:].rearrange("p (i c) -> p i c", i=2))

        def store_out(i, ch):
            c0, c1 = CHUNKS[ch]
            src = o_f32[i, 0][:] if ch == 0 else o_f32[i, 1][:, ch - 1, :, :]
            nc.sync.dma_start(out=out[P * i : P * i + 2 * P, c0:c1].rearrange("(i p) c -> p i c", i=2), in_=src)

        def round_out(i, f, engine="v"):
            o_bf[i, f] = work.tile([P, 2, 2, P, 2], BF16, name="o16", bufs=6, align_bytes=64)
            for n in range(2):
                dst = o_bf[i, f][:, n, :, :, :]
                if f == 0:
                    src = o_bank[i, 0][n][:] if engine == "s" else o_f32[i, f][:, n, :]
                    copy(engine, dst, src.rearrange("p (m u e) -> p u m e", u=2, e=2))
                else:
                    src = o_f32[i, f][:, :, n, :]
                    copy(
                        engine,
                        dst.rearrange("p u (q m) e -> p u q m e", q=2),
                        src.rearrange("p q (m u e) -> p u q m e", u=2, e=2),
                    )

        pl_codes = {}
        for f in range(2):
            pl_codes[f] = keep.tile([P, D], U32, name=f"plc_{f}", align_bytes=64)
        pl_scales = keep.tile([P, 2, D], U8, name="pls", align_bytes=64)
        pl_grp = {}

        def plane_turn(i, f, engine):
            xt = psum.tile([P, 2, 2, P], F32, name="pt", tag="tr", bufs=2)
            for n in range(2):
                for e in range(2):
                    w = o_bf[i, f][:, n, e, :, :].rearrange("p m e -> p (m e)").bitcast(F32)
                    nc.tensor.transpose(xt[:, n, e, :], w, ident[:])
            grp = work.tile([P, 2 * P, PACK], BF16, name="pg", bufs=4, align_bytes=64)
            pl_grp[i, f] = grp
            dst = grp[:].rearrange("p d t -> p (d t)").bitcast(F32).rearrange("p (i d e) -> p i d e", i=2, e=2)
            copy(engine, dst, xt[:].rearrange("p i e d -> p i d e"))

        def plane_quant(i, f):
            cols = slice(P * i, P * i + 2 * P)
            nc.vector.quantize_mx(
                out=pl_codes[f][:, cols].bitcast(FP8X4),
                scales=pl_scales[:, f, cols],
                in_=pl_grp[i, f][:].rearrange("p d t -> p (d t)"),
            )

        def store_words(f, i0, i1):
            nc.sync.dma_start(
                out=words[f, :, P * i0 : P * i1, :].rearrange("p d t -> p (d t)").bitcast(I32),
                in_=pl_codes[f][:, P * i0 : P * i1].bitcast(I32),
            )

        def store_scales():
            for q in range(4):
                nc.sync.dma_start(
                    out=scales[:, 4 * q : 4 * q + 4, :].bitcast(I32).rearrange("f r m -> r f m"),
                    in_=pl_scales[32 * q : 32 * q + 4, :, :].bitcast(I32),
                )

        mult(0, 0, 0)
        make_ab()
        sk_turn(0, 0, 0, "b")
        sk_turn(0, 0, 1, "b")
        inter(0, 0, 0, "v")
        sk_turn(0, 1, 0, "b")
        sk_turn(0, 1, 1, "b")
        quant_q(0, 0, 0)
        mult(0, 1, 0)
        inter(0, 1, 0, "v", 0, 256)
        inter(0, 1, 0, "s", 256, 512)
        quant_s(0, 0)
        quant_q(0, 1, 0, 0, 256)
        quant_s(0, 1)
        mult(1, 0, 0)
        quant_q(0, 1, 0, 256, 512)
        inter(1, 0, 0)
        for s in range(4):
            stage1(0, s)
        sk_turn(1, 0, 0, "tr")
        sk_turn(1, 0, 1, "tr")
        weigh(0, 0)
        weigh(0, 1)
        mult(1, 1, 0)
        weigh(0, 2)
        weigh(0, 3)
        sk_turn(1, 1, 0, "b")
        sk_turn(1, 1, 1, "b")
        inter(1, 1, 0)
        quant_q(1, 0, 0)
        mult(0, 0, 1)
        quant_s(1, 0)
        quant_s(1, 1)
        quant_q(1, 1, 0)
        for s in range(4):
            stage1(1, s)
        inter(0, 0, 1)
        quant_lr(0, 0)
        mult(0, 1, 1)
        inter(0, 1, 1)
        weigh(1, 0)
        weigh(1, 1)
        mult(1, 0, 1)
        quant_q(0, 0, 1)
        weigh(1, 2)
        quant_q(0, 1, 1)
        stage1(0, 4)
        stage1(0, 5)
        weigh(1, 3)
        inter(1, 0, 1)
        mult(1, 1, 1, "vvss")
        inter(1, 1, 1)
        weigh(0, 4, (0,))
        quant_lr(1, 0)
        weigh(0, 4, (1,))
        weigh(0, 5)
        quant_q(1, 0, 1)
        for i in (0, 2):
            stage2(i, 0)
            emit_out(i, 0)
            store_out(i, 0)
            round_out(i, 0, engine="s")
        stage1(0, 6)
        quant_lr(0, 1)
        quant_q(1, 1, 1)
        weigh(0, 6)
        stage1(1, 4)
        stage1(1, 5)
        stage1(0, 7)
        plane_turn(0, 0, "s")
        weigh(1, 4)
        weigh(1, 5)
        quant_lr(1, 1)
        plane_turn(2, 0, "s")
        weigh(0, 7)
        stage1(1, 6)
        stage2(4, 0)
        emit_out(4, 0)
        store_out(4, 0)
        round_out(4, 0, engine="s")
        stage2(0, 1)
        emit_out(0, 1)
        store_out(0, 1)
        stage1(1, 7)
        weigh(1, 6, (0,))
        quant_lr(0, 2)
        weigh(1, 7, (0,))
        for i in (2, 4):
            stage2(i, 1)
            emit_out(i, 1)
            store_out(i, 1)
        plane_turn(4, 0, "s")
        plane_quant(0, 0)
        quant_lr(1, 2, (0,))
        weigh(1, 6, (1,))
        weigh(1, 7, (1,))
        stage2(6, 0)
        stage2(6, 1)
        plane_quant(2, 0)
        store_words(0, 0, 4)
        quant_lr(1, 2, (1,))
        emit_out(6, 0)
        store_out(6, 0)
        emit_out(6, 1)
        store_out(6, 1)
        stage2(0, 2)
        round_out(6, 0)
        plane_quant(4, 0)
        emit_out(0, 2)
        store_out(0, 2)
        stage2(2, 2)
        emit_out(2, 2)
        store_out(2, 2)
        stage2(4, 2)
        round_out(0, 1)
        plane_turn(6, 0, "v")
        emit_out(4, 2)
        store_out(4, 2)
        stage2(6, 2)
        round_out(2, 1)
        emit_out(6, 2)
        store_out(6, 2)
        plane_turn(0, 1, "s")
        plane_quant(6, 0)
        store_words(0, 4, 8)
        round_out(4, 1)
        plane_turn(2, 1, "s")
        round_out(6, 1)
        plane_quant(0, 1)
        plane_turn(4, 1, "s")
        plane_turn(6, 1, "s")
        plane_quant(2, 1)
        store_words(1, 0, 4)
        plane_quant(4, 1)
        plane_quant(6, 1)
        store_words(1, 4, 8)
        store_scales()
